import numpy as np
import ml_dtypes


def mxq(x, axis, fmt="e4m3"):
    dtype, down = {"e4m3": (ml_dtypes.float8_e4m3fn, 7), "e5m2": (ml_dtypes.float8_e5m2, 14)}[fmt]
    v = np.moveaxis(np.asarray(x, np.float32).astype(ml_dtypes.bfloat16).astype(np.float64), axis, -1)
    blocks = v.reshape(v.shape[:-1] + (-1, 32))
    amax = np.abs(blocks).max(-1, keepdims=True)
    byte = np.maximum(np.where(amax > 0, np.frexp(amax)[1] - 1 + 127, 0) - down, 1)
    scale = np.exp2(byte - 127.0)
    codes = (blocks / scale).astype(np.float32).astype(dtype).astype(np.float64)
    return np.moveaxis((codes * scale).reshape(v.shape), -1, axis)


WIDE = False


def mx_kscale(k):
    if not WIDE:
        return np.ones(k)
    levels = np.array([24, -24, 12, -12, 0])
    if k % 512:
        return np.exp2(np.random.permutation(np.resize(levels, k // 32))).repeat(32)
    a = np.empty((k // 512, 16))
    for p in range(k // 512):
        a[p, :8] = np.random.permutation(np.resize(levels, 8))
        for g in range(8):
            far = levels[np.abs(levels - a[p, g]) >= 10]
            a[p, g + 8] = far[np.random.randint(len(far))]
    return np.exp2(a.ravel()).repeat(32)


def f64(x):
    return np.asarray(x).astype(np.float64)


def striped(idx):
    return np.tile(idx.reshape(-1, 16).T, (8, 1)).astype(np.uint16)


def unstriped(offs):
    return offs[:16].T.reshape(-1).astype(np.int64)


E2M1 = np.array([0.0, 0.5, 1.0, 1.5, 2.0, 3.0, 4.0, 6.0, -0.0, -0.5, -1.0, -1.5, -2.0, -3.0, -4.0, -6.0])


def pack_weight(w, fmt):
    k, n = w.shape
    w = f64(np.asarray(w, np.float32).astype(ml_dtypes.bfloat16)).reshape(k // 32, 32, n)
    amax = np.abs(w).max(1)
    if fmt == "e4m3":
        byte = np.frexp(amax)[1] - 1 + 127 - 7
    else:
        mant, ex = np.frexp(amax / 6.0)
        byte = np.where(mant > 0.5, ex, ex - 1) + 127
    byte = np.clip(np.where(amax > 0, byte, 1), 1, 254)
    scaled = (w * np.exp2(127.0 - byte)[:, None, :]).reshape(k, n).astype(np.float32)
    by_word = np.ascontiguousarray(scaled.reshape(k // 512, 128, 4, n).transpose(0, 1, 3, 2))
    if fmt == "e4m3":
        words = by_word.astype(ml_dtypes.float8_e4m3fn).view(np.uint8)
    else:
        c = by_word.astype(ml_dtypes.float4_e2m1fn).view(np.uint8) & 0xF
        words = (c[..., 0::2] | (c[..., 1::2] << 4)).reshape(k // 512, 128, 2 * n)
    return np.ascontiguousarray(words), np.ascontiguousarray(byte.astype(np.uint8).reshape(k // 512, 16, n))


def unpack_weight(words, scales, fmt):
    g, _, n = scales.shape
    words = np.ascontiguousarray(words).reshape(g, 128, n, -1)
    if fmt == "e4m3":
        vals = words.view(ml_dtypes.float8_e4m3fn).astype(np.float64)
    else:
        nib = np.empty((g, 128, n, 4), np.uint8)
        nib[..., 0::2] = words & 0xF
        nib[..., 1::2] = words >> 4
        vals = E2M1[nib]
    vals = vals * np.repeat(np.exp2(scales.astype(np.float64) - 127.0), 8, axis=1)[..., None]
    return vals.transpose(0, 1, 3, 2).reshape(g * 512, n)


def pack_table4(v):
    words, scales = pack_weight(v, "e2m1")
    g, t = words.shape[0] // 2, v.shape[1]
    return np.ascontiguousarray(words.reshape(g, 2, 128, t, 2).transpose(0, 2, 3, 1, 4).reshape(g, 128, t, 4)), scales


def unpack_table4(words, scales):
    g, _, t, _ = words.shape
    return unpack_weight(words.reshape(g, 128, t, 2, 2).transpose(0, 3, 1, 2, 4).reshape(2 * g, 128, 2 * t), scales, "e2m1")


K, R, N, T, J = 1024, 1024, 256, 1024, 512


def setup_inputs():
    n = np.random.standard_normal
    s = mx_kscale(K)[:, None]
    u = mx_kscale(R)[:, None]
    p_tab = pack_table4(n((K, T)) * s)
    p_wg = pack_weight(n((K, R)) / np.sqrt(K) / s, "e2m1")
    p_wu = pack_weight(n((K, R)) / np.sqrt(K) / s * u.T, "e2m1")
    return {
        "tab_words": p_tab[0],
        "tab_scales": p_tab[1],
        "wg_words": p_wg[0],
        "wg_scales": p_wg[1],
        "wu_words": p_wu[0],
        "wu_scales": p_wu[1],
        "wd": (n((R, N)) / np.sqrt(R) / u).astype(np.float32),
        "gT": (n((N, T))).astype(np.float32),
        "offs": striped(np.random.permutation(T)[:J]),
    }


def reference(tab_words, tab_scales, wg_words, wg_scales, wu_words, wu_scales, wd, gT, offs):
    idx = unstriped(offs)
    tab_ = unpack_table4(tab_words, tab_scales)[:, idx]
    wg_ = unpack_weight(wg_words, wg_scales, "e2m1")
    wu_ = unpack_weight(wu_words, wu_scales, "e2m1")
    ga = wg_.T @ tab_
    ub = wu_.T @ tab_
    h = np.tanh(ga) * ub
    h_ = mxq(h, 0, "e4m3")
    wd_ = mxq(f64(wd), 0, "e4m3")
    y = wd_.T @ h_
    return y * f64(gT)[:, idx]

@@ -1,0 +1,225 @@
+from contextlib import ExitStack
+
+import concourse.mybir as mybir
+from concourse.masks import make_identity
+
+K, R, N, T, J = 1024, 1024, 256, 1024, 512
+FLOPS = 2 * 2 * K * R * J + 2 * R * N * J
+
+F32 = mybir.dt.float32
+BF16 = mybir.dt.bfloat16
+I32 = mybir.dt.int32
+U32 = mybir.dt.uint32
+U16 = mybir.dt.uint16
+U8 = mybir.dt.uint8
+FP8X4 = mybir.dt.float8_e4m3fn_x4
+FP4X4 = mybir.dt.float4_e2m1fn_x4
+MULT = mybir.AluOpType.mult
+TANH = mybir.ActivationFunctionType.Tanh
+
+P = 128
+HALF = 512
+
+
+def tile_list_gmlpt_tanh_gate_kernel(
+    tc, tab_words, tab_scales, wg_words, wg_scales, wu_words, wu_scales, wd, gT, offs, out
+):
+    nc = tc.nc
+    with ExitStack() as ctx:
+        keep = ctx.enter_context(tc.tile_pool(name="keep", bufs=1))
+        ring = ctx.enter_context(tc.tile_pool(name="ring", bufs=3))
+        psum = ctx.enter_context(tc.psum_pool(name="psum", bufs=1))
+
+        offsets = keep.tile([P, J // 16], U16, name="offsets")
+        tab_w = keep.tile([P, T], I32, name="tab_w", tag="table_words", align_bytes=64)
+        tab_s = keep.tile([P, 2, T // 4], I32, name="tab_s", tag="table_scales", align_bytes=64)
+        w_s = keep.tile([P, 2, 2, R // 4], I32, name="w_s", align_bytes=64)
+        w_early = keep.tile([P, 2, 2, HALF // 2], I32, name="w_early", align_bytes=64)
+        ident = keep.tile([P, P], F32, name="ident", align_bytes=64)
+        warm_in = keep.tile([P, 1], F32, name="warm_in", tag="late_words", align_bytes=64)
+        warm_out = keep.tile([P, 1], F32, name="warm_out", tag="late_wd", align_bytes=64)
+
+        def load_scales(dst, src):
+            rows = src.bitcast(I32).rearrange("a (q r) c -> r q a c", r=4)
+            for r in range(4):
+                nc.sync.dma_start(out=dst[r:P:32], in_=rows[r])
+
+        def load_words(queue, dst, m, b):
+            src = (wg_words, wu_words)[m].bitcast(I32).rearrange("a p c -> p a c")
+            queue.dma_start(out=dst[:, m], in_=src[:, :, b * (HALF // 2) : (b + 1) * (HALF // 2)])
+
+        nc.vector.memset(tab_s[:], 0)
+        nc.vector.memset(warm_in[:], 0.0)
+        nc.vector.memset(w_s[:, 0], 0)
+        nc.vector.memset(w_s[:, 1], 0)
+        nc.scalar.activation(out=warm_out[:], in_=warm_in[:], func=TANH)
+        load_words(nc.gpsimd, w_early, 0, 0)
+        load_words(nc.gpsimd, w_early, 1, 0)
+        make_identity(nc, ident[:])
+
+        nc.sync.dma_start(offsets[:], offs)
+        nc.sync.dma_start(out=tab_w[:], in_=tab_words[0].rearrange("p t d -> p (t d)").bitcast(I32))
+        load_scales(tab_s, tab_scales)
+        load_scales(w_s[:, 0], wg_scales)
+        load_scales(w_s[:, 1], wu_scales)
+        w_late = keep.tile([P, 2, 2, HALF // 2], I32, name="w_late", tag="late_words", align_bytes=64)
+        wd_raw = keep.tile([P, 2, 4, N], F32, name="wd_raw", tag="late_wd", align_bytes=64)
+        load_words(nc.sync, w_late, 0, 1)
+        load_words(nc.sync, w_late, 1, 1)
+        wd_rows = wd.rearrange("(b p t) n -> b p t n", b=2, t=4)
+        for b in range(2):
+            nc.sync.dma_start(out=wd_raw[:, b], in_=wd_rows[b])
+        w_w = (w_early, w_late)
+
+        picked_w = keep.tile([P, J], U32, name="picked_w", align_bytes=64)
+        picked_s = keep.tile([P, 2, J], U8, name="picked_s", align_bytes=64)
+        parted = keep.tile([P, 2, 2 * J], U8, name="parted", align_bytes=64)
+        tab_s8 = tab_s[:].bitcast(U8)
+        w_s8 = w_s[:].bitcast(U8)
+
+        def lst(j0, j1):
+            return offsets[:, j0 // 16 : j1 // 16]
+
+        def pick(j0, j1):
+            nc.vector.tensor_copy(out=picked_w[:, j0:j1], in_=tab_w[:].bitcast(U32).indirect(lst(j0, j1)))
+            nc.vector.tensor_copy(out=picked_s[:, 0, j0:j1], in_=tab_s8[:, 0, :].indirect(lst(j0, j1)))
+            nc.vector.tensor_copy(
+                out=parted[:, :, 2 * j0 : 2 * j1].bitcast(U16),
+                in_=picked_w[:, j0:j1].bitcast(U16).rearrange("p (j d) -> p d j", d=2),
+            )
+            nc.vector.tensor_copy(out=picked_s[:, 1, j0:j1], in_=tab_s8[:, 1, :].indirect(lst(j0, j1)))
+
+        h_rows = keep.tile([P, 4, 2, HALF], BF16, name="h_rows", align_bytes=64)
+
+        def first_layer(jt, b):
+            banks = [
+                psum.tile([P, HALF], F32, name="ga", tag="ga", bufs=2),
+                psum.tile([P, HALF], F32, name="ub", tag="ub", bufs=3),
+            ]
+            for m in range(2):
+                for a in range(2):
+                    nc.tensor.matmul_mx(
+                        out=banks[m][:],
+                        lhsT=parted[:, a, 2 * P * jt : 2 * P * (jt + 1)].bitcast(FP4X4),
+                        lhsT_scale=picked_s[:, a, P * jt : P * (jt + 1)],
+                        rhs=w_w[b][:, m, a, :].bitcast(U8).bitcast(FP4X4),
+                        rhs_scale=w_s8[:, m, a, HALF * b : HALF * (b + 1)],
+                        start=(a == 0),
+                        stop=(a == 1),
+                    )
+            th = ring.tile([P, 2, P, 2], F32, name="th")
+            nc.scalar.activation(out=th[:], in_=banks[0][:].rearrange("j (p u e) -> j u p e", u=2, e=2), func=TANH)
+            nc.vector.tensor_tensor(
+                out=h_rows[:, jt, b, :].rearrange("j (u p e) -> j u p e", u=2, e=2),
+                in0=banks[1][:].rearrange("j (p u e) -> j u p e", u=2, e=2),
+                in1=th[:],
+                op=MULT,
+            )
+
+        h_cols = keep.tile([P, 2, J, 4], BF16, name="h_cols", align_bytes=64)
+        h_codes = keep.tile([P, 2, J], U32, name="h_codes", align_bytes=64)
+        h_scales = keep.tile([P, 2, J], U8, name="h_scales", align_bytes=64)
+
+        def turn(jt, halves):
+            turned = psum.tile([P, 2, 2, P], F32, name="turned", tag="turned", bufs=2)
+            words = h_rows[:].bitcast(F32)
+            for b in halves:
+                for u in range(2):
+                    nc.tensor.transpose(turned[:, b, u, :], words[:, jt, b, P * u : P * (u + 1)], ident[:])
+            b0, b1 = halves[0], halves[-1] + 1
+            nc.scalar.copy(
+                out=h_cols[:].bitcast(F32)[:, b0:b1, P * jt : P * (jt + 1), :],
+                in_=turned[:, b0:b1].rearrange("p b u j -> p b j u"),
+            )
+
+        def quantise_h(b, j0, j1):
+            nc.vector.quantize_mx(
+                out=h_codes[:, b, j0:j1].bitcast(FP8X4),
+                scales=h_scales[:, b, j0:j1],
+                in_=h_cols[:, b, j0:j1, :].rearrange("p j t -> p (j t)"),
+            )
+
+        wd_bf = keep.tile([P, 2, N, 4], BF16, name="wd_bf", align_bytes=64)
+        wd_codes = keep.tile([P, 2, N], U32, name="wd_codes", align_bytes=64)
+        wd_scales = keep.tile([P, 2, N], U8, name="wd_scales", align_bytes=64)
+
+        def round_wd(b, c):
+            cols = slice(P * c, P * (c + 1))
+            nc.scalar.copy(out=wd_bf[:, b, cols, :], in_=wd_raw[:, b, :, cols].rearrange("p t n -> p n t"))
+
+        def quantise_wd(b):
+            nc.vector.quantize_mx(
+                out=wd_codes[:, b, :].bitcast(FP8X4),
+                scales=wd_scales[:, b, :],
+                in_=wd_bf[:, b].rearrange("p n t -> p (n t)"),
+            )
+
+        out_view = out.rearrange("(c p) j -> p c j", c=2)
+
+        def second_layer(j0, j1):
+            y = psum.tile([P, 2, j1 - j0], F32, name="y", tag="y", bufs=1)
+            for c in range(2):
+                for b in range(2):
+                    nc.tensor.matmul_mx(
+                        out=y[:, c, :],
+                        lhsT=wd_codes[:, b, P * c : P * (c + 1)].bitcast(FP8X4),
+                        lhsT_scale=wd_scales[:, b, P * c : P * (c + 1)],
+                        rhs=h_codes[:, b, j0:j1].bitcast(FP8X4),
+                        rhs_scale=h_scales[:, b, j0:j1],
+                        start=(b == 0),
+                        stop=(b == 1),
+                    )
+            return y
+
+        def finish_fused(y, j0, j1):
+            y_sb = keep.tile([P, 2, j1 - j0], F32, name=f"y_sb{j0}")
+            res = keep.tile([P, 2, j1 - j0], F32, name=f"res{j0}")
+            nc.scalar.copy(out=y_sb[:], in_=y[:])
+            for c in range(2):
+                nc.vector.tensor_tensor(out=res[:, c, :], in0=gate[c][:].indirect(lst(j0, j1)), in1=y_sb[:, c, :], op=MULT)
+            nc.sync.dma_start(out=out_view[:, :, j0:j1], in_=res[:])
+
+        gate = []
+        pick(0, 128)
+        pick(128, 256)
+        first_layer(0, 0)
+        first_layer(1, 0)
+        pick(256, 384)
+        first_layer(0, 1)
+        pick(384, 512)
+        for c, tag in enumerate(("table_words", "table_scales")):
+            gate.append(keep.tile([P, T], F32, name=f"gate{c}", tag=tag, align_bytes=64))
+            nc.sync.dma_start(out=gate[c][:], in_=gT[c * P : (c + 1) * P, :])
+        first_layer(1, 1)
+        round_wd(0, 0)
+        round_wd(0, 1)
+        first_layer(2, 0)
+        quantise_wd(0)
+        turn(0, (0, 1))
+        turn(1, (0, 1))
+        round_wd(1, 0)
+        round_wd(1, 1)
+        quantise_h(0, 0, 256)
+        first_layer(2, 1)
+        quantise_h(1, 0, 256)
+        quantise_wd(1)
+        first_layer(3, 0)
+        y = second_layer(0, 256)
+        turn(2, (0, 1))
+        finish_fused(y, 0, 256)
+        quantise_h(0, 256, 384)
+        quantise_h(1, 256, 384)
+        first_layer(3, 1)
+        turn(3, (0,))
+        last_gate = keep.tile([P, 2, P], F32, name="last_gate")
+        for c in range(2):
+            nc.vector.tensor_copy(out=last_gate[:, c, :], in_=gate[c][:].indirect(lst(384, 512)))
+        quantise_h(0, 384, 512)
+        y = second_layer(256, 384)
+        turn(3, (1,))
+        quantise_h(1, 384, 512)
+        finish_fused(y, 256, 384)
+        y = second_layer(384, 512)
+        res = keep.tile([P, 2, P], F32, name="res_last")
+        nc.vector.tensor_tensor(out=res[:], in0=y[:], in1=last_gate[:], op=MULT)
+        nc.sync.dma_start(out=out_view[:, :, 384:512], in_=res[:])

@@ -27,109 +27,129 @@ def tile_list_gmlpt_tanh_gate_kernel(
     nc = tc.nc
     with ExitStack() as ctx:
         keep = ctx.enter_context(tc.tile_pool(name="keep", bufs=1))
-        ring = ctx.enter_context(tc.tile_pool(name="ring", bufs=3))
+        placed = ctx.enter_context(tc.tile_pool(name="placed", bufs=1))
         psum = ctx.enter_context(tc.psum_pool(name="psum", bufs=1))
 
+        def sb(shape, dtype, name, tag=None):
+            return keep.tile(shape, dtype, name=name, tag=tag or name, align_bytes=64)
+
         offsets = keep.tile([P, J // 16], U16, name="offsets")
-        tab_w = keep.tile([P, T], I32, name="tab_w", tag="table_words", align_bytes=64)
-        tab_s = keep.tile([P, 2, T // 4], I32, name="tab_s", tag="table_scales", align_bytes=64)
-        w_s = keep.tile([P, 2, 2, R // 4], I32, name="w_s", align_bytes=64)
-        w_early = keep.tile([P, 2, 2, HALF // 2], I32, name="w_early", align_bytes=64)
-        ident = keep.tile([P, P], F32, name="ident", align_bytes=64)
-        warm_in = keep.tile([P, 1], F32, name="warm_in", tag="late_words", align_bytes=64)
-        warm_out = keep.tile([P, 1], F32, name="warm_out", tag="late_wd", align_bytes=64)
+        tab_s = sb([P, 2, T // 4], I32, "tab_s")
+        wg_early = sb([P, 2, HALF // 2], I32, "wg_early")
+        ident = sb([P, P], F32, "ident")
+        zero_in = sb([P, 1], F32, "zero_in")
+        zero = sb([P, 1], F32, "zero")
+
+        def at(offset, shape, dtype, name):
+            return placed.tile(shape, dtype, name=name, offset=offset, align_bytes=64)
 
         def load_scales(dst, src):
-            rows = src.bitcast(I32).rearrange("a (q r) c -> r q a c", r=4)
-            for r in range(4):
-                nc.sync.dma_start(out=dst[r:P:32], in_=rows[r])
+            rows = src.bitcast(I32).rearrange("a (q r) c -> q r a c", r=4)
+            for q in range(4):
+                nc.sync.dma_start(out=dst[32 * q : 32 * q + 4], in_=rows[q])
 
-        def load_words(queue, dst, m, b):
+        def load_words(dst, m, b):
             src = (wg_words, wu_words)[m].bitcast(I32).rearrange("a p c -> p a c")
-            queue.dma_start(out=dst[:, m], in_=src[:, :, b * (HALF // 2) : (b + 1) * (HALF // 2)])
+            nc.sync.dma_start(out=dst, in_=src[:, :, b * (HALF // 2) : (b + 1) * (HALF // 2)])
 
-        nc.vector.memset(tab_s[:], 0)
-        nc.vector.memset(warm_in[:], 0.0)
-        nc.vector.memset(w_s[:, 0], 0)
-        nc.vector.memset(w_s[:, 1], 0)
-        nc.scalar.activation(out=warm_out[:], in_=warm_in[:], func=TANH)
-        load_words(nc.gpsimd, w_early, 0, 0)
-        load_words(nc.gpsimd, w_early, 1, 0)
+        tab_w = sb([P, T], I32, "tab_w")
+        w_s = [sb([P, 2, R // 4], I32, f"w_s{m}") for m in range(2)]
+        wu_early = sb([P, 2, HALF // 2], I32, "wu_early")
+        w_late = sb([P, 2, 2, HALF // 2], I32, "w_late")
+        gate = sb([P, 2, T], F32, "gate")
+        wd_raw = [sb([P, 4, N], F32, f"wd_raw{b}") for b in range(2)]
+        nc.vector.memset(tab_s[:, 0], 0)
+        nc.gpsimd.memset(tab_s[:, 1], 0)
+        nc.vector.memset(zero_in[:], 0.0)
+        nc.scalar.activation(out=zero[:], in_=zero_in[:], func=TANH)
+        nc.vector.memset(w_s[0][:], 0)
+        nc.gpsimd.memset(w_s[1][:], 0)
         make_identity(nc, ident[:])
 
         nc.sync.dma_start(offsets[:], offs)
-        nc.sync.dma_start(out=tab_w[:], in_=tab_words[0].rearrange("p t d -> p (t d)").bitcast(I32))
+        load_words(wg_early[:], 0, 0)
         load_scales(tab_s, tab_scales)
-        load_scales(w_s[:, 0], wg_scales)
-        load_scales(w_s[:, 1], wu_scales)
-        w_late = keep.tile([P, 2, 2, HALF // 2], I32, name="w_late", tag="late_words", align_bytes=64)
-        wd_raw = keep.tile([P, 2, 4, N], F32, name="wd_raw", tag="late_wd", align_bytes=64)
-        load_words(nc.sync, w_late, 0, 1)
-        load_words(nc.sync, w_late, 1, 1)
+        nc.sync.dma_start(out=tab_w[:], in_=tab_words[0].rearrange("p t d -> p (t d)").bitcast(I32))
+        load_scales(w_s[0], wg_scales)
+        load_words(wu_early[:], 1, 0)
+        for c in range(2):
+            nc.sync.dma_start(out=gate[:, c, :], in_=gT[c * P : (c + 1) * P, :])
+        load_scales(w_s[1], wu_scales)
         wd_rows = wd.rearrange("(b p t) n -> b p t n", b=2, t=4)
-        for b in range(2):
-            nc.sync.dma_start(out=wd_raw[:, b], in_=wd_rows[b])
-        w_w = (w_early, w_late)
+        nc.sync.dma_start(out=wd_raw[0][:], in_=wd_rows[0])
+        for m in range(2):
+            load_words(w_late[:, m], m, 1)
+        nc.sync.dma_start(out=wd_raw[1][:], in_=wd_rows[1])
+        w_w = [[wg_early[:], w_late[:, 0]], [wu_early[:], w_late[:, 1]]]
 
-        picked_w = keep.tile([P, J], U32, name="picked_w", align_bytes=64)
-        picked_s = keep.tile([P, 2, J], U8, name="picked_s", align_bytes=64)
-        parted = keep.tile([P, 2, 2 * J], U8, name="parted", align_bytes=64)
         tab_s8 = tab_s[:].bitcast(U8)
-        w_s8 = w_s[:].bitcast(U8)
 
         def lst(j0, j1):
             return offsets[:, j0 // 16 : j1 // 16]
 
-        def pick(j0, j1):
-            nc.vector.tensor_copy(out=picked_w[:, j0:j1], in_=tab_w[:].bitcast(U32).indirect(lst(j0, j1)))
-            nc.vector.tensor_copy(out=picked_s[:, 0, j0:j1], in_=tab_s8[:, 0, :].indirect(lst(j0, j1)))
-            nc.vector.tensor_copy(
-                out=parted[:, :, 2 * j0 : 2 * j1].bitcast(U16),
-                in_=picked_w[:, j0:j1].bitcast(U16).rearrange("p (j d) -> p d j", d=2),
-            )
-            nc.vector.tensor_copy(out=picked_s[:, 1, j0:j1], in_=tab_s8[:, 1, :].indirect(lst(j0, j1)))
+        stat_w, stat_s = {}, {}
 
-        h_rows = keep.tile([P, 4, 2, HALF], BF16, name="h_rows", align_bytes=64)
+        def pick_scales(j0, j1, picked):
+            for a in range(2):
+                nc.vector.tensor_copy(out=picked[:, a, :], in_=tab_s8[:, a, :].indirect(lst(j0, j1)))
+            for jt in range(j0 // P, j1 // P):
+                stat_s[jt] = picked[:, :, P * jt - j0 : P * (jt + 1) - j0]
 
-        def first_layer(jt, b):
-            banks = [
-                psum.tile([P, HALF], F32, name="ga", tag="ga", bufs=2),
-                psum.tile([P, HALF], F32, name="ub", tag="ub", bufs=3),
-            ]
-            for m in range(2):
-                for a in range(2):
-                    nc.tensor.matmul_mx(
-                        out=banks[m][:],
-                        lhsT=parted[:, a, 2 * P * jt : 2 * P * (jt + 1)].bitcast(FP4X4),
-                        lhsT_scale=picked_s[:, a, P * jt : P * (jt + 1)],
-                        rhs=w_w[b][:, m, a, :].bitcast(U8).bitcast(FP4X4),
-                        rhs_scale=w_s8[:, m, a, HALF * b : HALF * (b + 1)],
-                        start=(a == 0),
-                        stop=(a == 1),
-                    )
-            th = ring.tile([P, 2, P, 2], F32, name="th")
-            nc.scalar.activation(out=th[:], in_=banks[0][:].rearrange("j (p u e) -> j u p e", u=2, e=2), func=TANH)
+        def pick_words(j0, j1, picked):
+            parted = sb([P, 2, 2 * (j1 - j0)], U8, f"parted{j0}")
+            nc.vector.tensor_copy(out=picked[:], in_=tab_w[:].bitcast(U32).indirect(lst(j0, j1)))
+            nc.vector.tensor_copy(out=parted[:].bitcast(U16), in_=picked[:].bitcast(U16).rearrange("p (j d) -> p d j", d=2))
+            for jt in range(j0 // P, j1 // P):
+                stat_w[jt] = parted[:, :, 2 * (P * jt - j0) : 2 * (P * (jt + 1) - j0)]
+
+        h_rows = [sb([P, 2, HALF], BF16, f"h_rows{jt}") for jt in range(4)]
+        th = {}
+
+        def product(m, jt, b, bank):
+            for a in range(2):
+                nc.tensor.matmul_mx(
+                    out=bank[:],
+                    lhsT=stat_w[jt][:, a, :].bitcast(FP4X4),
+                    lhsT_scale=stat_s[jt][:, a, :],
+                    rhs=w_w[m][b][:, a, :].bitcast(U8).bitcast(FP4X4),
+                    rhs_scale=w_s[m][:].bitcast(U8)[:, a, HALF * b : HALF * (b + 1)],
+                    start=(a == 0),
+                    stop=(a == 1),
+                )
+
+        def gate_half(jt, b):
+            ga = psum.tile([P, HALF], F32, name="ga", tag="ga", bufs=2)
+            product(0, jt, b, ga)
+            th[jt, b] = sb([P, 2, P, 2], F32, f"th{jt}{b}")
+            nc.scalar.activation(out=th[jt, b][:], in_=ga[:].rearrange("j (p u e) -> j u p e", u=2, e=2), func=TANH, bias=zero[:])
+
+        def up_half(jt, b):
+            ub = psum.tile([P, HALF], F32, name="ub", tag="ub", bufs=3)
+            product(1, jt, b, ub)
             nc.vector.tensor_tensor(
-                out=h_rows[:, jt, b, :].rearrange("j (u p e) -> j u p e", u=2, e=2),
-                in0=banks[1][:].rearrange("j (p u e) -> j u p e", u=2, e=2),
-                in1=th[:],
+                out=h_rows[jt][:, b, :].rearrange("j (u p e) -> j u p e", u=2, e=2),
+                in0=ub[:].rearrange("j (p u e) -> j u p e", u=2, e=2),
+                in1=th[jt, b][:],
                 op=MULT,
             )
 
-        h_cols = keep.tile([P, 2, J, 4], BF16, name="h_cols", align_bytes=64)
-        h_codes = keep.tile([P, 2, J], U32, name="h_codes", align_bytes=64)
-        h_scales = keep.tile([P, 2, J], U8, name="h_scales", align_bytes=64)
+        def unit(jt, b):
+            gate_half(jt, b)
+            up_half(jt, b)
 
-        def turn(jt, halves):
+        h_cols = sb([P, 2, J, 4], BF16, "h_cols")
+        h_codes = sb([P, 2, J], U32, "h_codes")
+        h_scales = sb([P, 2, J], U8, "h_scales")
+
+        def turn(b, jt0, jt1):
             turned = psum.tile([P, 2, 2, P], F32, name="turned", tag="turned", bufs=2)
-            words = h_rows[:].bitcast(F32)
-            for b in halves:
+            for jt in range(jt0, jt1):
+                words = h_rows[jt][:].bitcast(F32)
                 for u in range(2):
-                    nc.tensor.transpose(turned[:, b, u, :], words[:, jt, b, P * u : P * (u + 1)], ident[:])
-            b0, b1 = halves[0], halves[-1] + 1
+                    nc.tensor.transpose(turned[:, jt - jt0, u, :], words[:, b, P * u : P * (u + 1)], ident[:])
             nc.scalar.copy(
-                out=h_cols[:].bitcast(F32)[:, b0:b1, P * jt : P * (jt + 1), :],
-                in_=turned[:, b0:b1].rearrange("p b u j -> p b j u"),
+                out=h_cols[:].bitcast(F32)[:, b, P * jt0 : P * jt1, :].rearrange("p (i j) u -> p i j u", j=P),
+                in_=turned[:, : jt1 - jt0].rearrange("p i u j -> p i j u"),
             )
 
         def quantise_h(b, j0, j1):
@@ -139,20 +159,23 @@ def tile_list_gmlpt_tanh_gate_kernel(
                 in_=h_cols[:, b, j0:j1, :].rearrange("p j t -> p (j t)"),
             )
 
-        wd_bf = keep.tile([P, 2, N, 4], BF16, name="wd_bf", align_bytes=64)
-        wd_codes = keep.tile([P, 2, N], U32, name="wd_codes", align_bytes=64)
-        wd_scales = keep.tile([P, 2, N], U8, name="wd_scales", align_bytes=64)
+        wd_codes = sb([P, 2, N], U32, "wd_codes")
+        wd_scales = sb([P, 2, N], U8, "wd_scales")
 
-        def round_wd(b, c):
+        def prepare_wd(b, c, tag):
             cols = slice(P * c, P * (c + 1))
-            nc.scalar.copy(out=wd_bf[:, b, cols, :], in_=wd_raw[:, b, :, cols].rearrange("p t n -> p n t"))
-
-        def quantise_wd(b):
+            wd_bf = sb([P, P, 4], BF16, f"wd_bf{b}{c}", tag)
+            nc.scalar.copy(out=wd_bf[:], in_=wd_raw[b][:, :, cols].rearrange("p t n -> p n t"))
             nc.vector.quantize_mx(
-                out=wd_codes[:, b, :].bitcast(FP8X4),
-                scales=wd_scales[:, b, :],
-                in_=wd_bf[:, b].rearrange("p n t -> p (n t)"),
+                out=wd_codes[:, b, cols].bitcast(FP8X4),
+                scales=wd_scales[:, b, cols],
+                in_=wd_bf[:].rearrange("p n t -> p (n t)"),
             )
+
+        picked_g = sb([P, 2, J], F32, "picked_g")
+
+        def pick_gate(c, j0, j1):
+            nc.vector.tensor_copy(out=picked_g[:, c, j0:j1], in_=gate[:, c, :].indirect(lst(j0, j1)))
 
         out_view = out.rearrange("(c p) j -> p c j", c=2)
 
@@ -169,57 +192,41 @@ def tile_list_gmlpt_tanh_gate_kernel(
                         start=(b == 0),
                         stop=(b == 1),
                     )
-            return y
-
-        def finish_fused(y, j0, j1):
-            y_sb = keep.tile([P, 2, j1 - j0], F32, name=f"y_sb{j0}")
-            res = keep.tile([P, 2, j1 - j0], F32, name=f"res{j0}")
-            nc.scalar.copy(out=y_sb[:], in_=y[:])
-            for c in range(2):
-                nc.vector.tensor_tensor(out=res[:, c, :], in0=gate[c][:].indirect(lst(j0, j1)), in1=y_sb[:, c, :], op=MULT)
+            res = sb([P, 2, j1 - j0], F32, f"res{j0}")
+            nc.vector.tensor_tensor(out=res[:], in0=y[:], in1=picked_g[:, :, j0:j1], op=MULT)
             nc.sync.dma_start(out=out_view[:, :, j0:j1], in_=res[:])
 
-        gate = []
-        pick(0, 128)
-        pick(128, 256)
-        first_layer(0, 0)
-        first_layer(1, 0)
-        pick(256, 384)
-        first_layer(0, 1)
-        pick(384, 512)
-        for c, tag in enumerate(("table_words", "table_scales")):
-            gate.append(keep.tile([P, T], F32, name=f"gate{c}", tag=tag, align_bytes=64))
-            nc.sync.dma_start(out=gate[c][:], in_=gT[c * P : (c + 1) * P, :])
-        first_layer(1, 1)
-        round_wd(0, 0)
-        round_wd(0, 1)
-        first_layer(2, 0)
-        quantise_wd(0)
-        turn(0, (0, 1))
-        turn(1, (0, 1))
-        round_wd(1, 0)
-        round_wd(1, 1)
+        pick_scales(0, 256, sb([P, 2, 256], U8, "picked_s0"))
+        pick_words(0, 128, sb([P, P], U32, "picked_w0"))
+        pick_words(128, 256, at(256, [P, P], U32, "picked_w1"))
+        gate_half(0, 0)
+        gate_half(1, 0)
+        pick_scales(256, 512, at(0, [P, 2, 256], U8, "picked_s1"))
+        pick_words(256, 512, at(512, [P, 2 * P], U32, "picked_w2"))
+        gate_half(2, 0)
+        gate_half(3, 0)
+        pick_gate(0, 0, 512)
+        pick_gate(1, 0, 512)
+        for jt in range(4):
+            up_half(jt, 0)
+        prepare_wd(0, 0, None)
+        prepare_wd(0, 1, None)
+        unit(0, 1)
+        prepare_wd(1, 0, None)
+        turn(0, 0, 2)
+        turn(0, 2, 4)
+        unit(1, 1)
         quantise_h(0, 0, 256)
-        first_layer(2, 1)
+        quantise_h(0, 256, 512)
+        unit(2, 1)
+        prepare_wd(1, 1, "th11")
+        turn(1, 0, 2)
+        unit(3, 1)
         quantise_h(1, 0, 256)
-        quantise_wd(1)
-        first_layer(3, 0)
-        y = second_layer(0, 256)
-        turn(2, (0, 1))
-        finish_fused(y, 0, 256)
-        quantise_h(0, 256, 384)
+        turn(1, 2, 3)
+        second_layer(0, 256)
+        turn(1, 3, 4)
         quantise_h(1, 256, 384)
-        first_layer(3, 1)
-        turn(3, (0,))
-        last_gate = keep.tile([P, 2, P], F32, name="last_gate")
-        for c in range(2):
-            nc.vector.tensor_copy(out=last_gate[:, c, :], in_=gate[c][:].indirect(lst(384, 512)))
-        quantise_h(0, 384, 512)
-        y = second_layer(256, 384)
-        turn(3, (1,))
+        second_layer(256, 384)
         quantise_h(1, 384, 512)
-        finish_fused(y, 256, 384)
-        y = second_layer(384, 512)
-        res = keep.tile([P, 2, P], F32, name="res_last")
-        nc.vector.tensor_tensor(out=res[:], in0=y[:], in1=last_gate[:], op=MULT)
-        nc.sync.dma_start(out=out_view[:, :, 384:512], in_=res[:])
+        second_layer(384, 512)

@@ -44,9 +44,9 @@ def tile_list_gmlpt_tanh_gate_kernel(
             return placed.tile(shape, dtype, name=name, offset=offset, align_bytes=64)
 
         def load_scales(dst, src):
-            rows = src.bitcast(I32).rearrange("a (q r) c -> q r a c", r=4)
-            for q in range(4):
-                nc.sync.dma_start(out=dst[32 * q : 32 * q + 4], in_=rows[q])
+            rows = src.bitcast(I32).rearrange("a (q r) c -> r q a c", r=4)
+            for r in range(4):
+                nc.sync.dma_start(out=dst[r:P:32], in_=rows[r])
 
         def load_words(dst, m, b):
             src = (wg_words, wu_words)[m].bitcast(I32).rearrange("a p c -> p a c")
@@ -55,7 +55,7 @@ def tile_list_gmlpt_tanh_gate_kernel(
         tab_w = sb([P, T], I32, "tab_w")
         w_s = [sb([P, 2, R // 4], I32, f"w_s{m}") for m in range(2)]
         wu_early = sb([P, 2, HALF // 2], I32, "wu_early")
-        w_late = sb([P, 2, 2, HALF // 2], I32, "w_late")
+        w_late = [sb([P, 2, HALF // 2], I32, f"w_late{m}") for m in range(2)]
         gate = sb([P, 2, T], F32, "gate")
         wd_raw = [sb([P, 4, N], F32, f"wd_raw{b}") for b in range(2)]
         nc.vector.memset(tab_s[:, 0], 0)
@@ -72,15 +72,16 @@ def tile_list_gmlpt_tanh_gate_kernel(
         nc.sync.dma_start(out=tab_w[:], in_=tab_words[0].rearrange("p t d -> p (t d)").bitcast(I32))
         load_scales(w_s[0], wg_scales)
         load_words(wu_early[:], 1, 0)
-        for c in range(2):
-            nc.sync.dma_start(out=gate[:, c, :], in_=gT[c * P : (c + 1) * P, :])
-        load_scales(w_s[1], wu_scales)
-        wd_rows = wd.rearrange("(b p t) n -> b p t n", b=2, t=4)
-        nc.sync.dma_start(out=wd_raw[0][:], in_=wd_rows[0])
         for m in range(2):
-            load_words(w_late[:, m], m, 1)
-        nc.sync.dma_start(out=wd_raw[1][:], in_=wd_rows[1])
-        w_w = [[wg_early[:], w_late[:, 0]], [wu_early[:], w_late[:, 1]]]
+            load_words(w_late[m][:], m, 1)
+        nc.sync.dma_start(out=gate[:, 0, :], in_=gT[:P, :])
+        load_scales(w_s[1], wu_scales)
+        nc.sync.dma_start(out=gate[:, 1, :], in_=gT[P:, :])
+        nc.sync.dma_start(out=wd_raw[0][:], in_=wd[:HALF].rearrange("(p t) n -> p t n", t=4))
+        late_rows = wd[HALF:].rearrange("(q t i) n -> t q i n", t=4, i=8)
+        for t in range(4):
+            nc.sync.dma_start(out=wd_raw[1][:, t, :], in_=late_rows[t])
+        w_early = [wg_early, wu_early]
 
         tab_s8 = tab_s[:].bitcast(U8)
 
@@ -102,61 +103,88 @@ def tile_list_gmlpt_tanh_gate_kernel(
             for jt in range(j0 // P, j1 // P):
                 stat_w[jt] = parted[:, :, 2 * (P * jt - j0) : 2 * (P * (jt + 1) - j0)]
 
-        h_rows = [sb([P, 2, HALF], BF16, f"h_rows{jt}") for jt in range(4)]
+        h_rows = [sb([P, HALF], BF16, f"h_rows{jt}") for jt in range(4)]
+        h_cols = [sb([P, J, 4], BF16, f"h_cols{b}") for b in range(2)]
+        h_codes = sb([P, 2, J], U32, "h_codes")
+        h_scales = sb([P, 2, J], U8, "h_scales")
+        dealt_w = [sb([P, 2, 4, P // 2], I32, f"dealt_w{m}") for m in range(2)]
+        dealt_s = [sb([P, 2, 4, P // 4], I32, f"dealt_s{m}") for m in range(2)]
         th = {}
 
-        def product(m, jt, b, bank):
+        def bank(shape):
+            return psum.tile(shape, F32, name="bank", tag="bank", bufs=8)
+
+        def deal(m):
+            nc.vector.tensor_copy(
+                out=dealt_s[m][:].rearrange("p a t (q e) -> p a t q e", e=2),
+                in_=w_s[m][:, :, HALF // 4 :].rearrange("p a (q t e) -> p a t q e", t=4, e=2),
+            )
+            nc.vector.tensor_copy(
+                out=dealt_w[m][:].rearrange("p a t (q e) -> p a t q e", e=4),
+                in_=w_late[m][:].rearrange("p a (q t e) -> p a t q e", t=4, e=4),
+            )
+
+        def early_product(m, jt):
+            acc = bank([P, HALF])
             for a in range(2):
                 nc.tensor.matmul_mx(
-                    out=bank[:],
+                    out=acc[:],
                     lhsT=stat_w[jt][:, a, :].bitcast(FP4X4),
                     lhsT_scale=stat_s[jt][:, a, :],
-                    rhs=w_w[m][b][:, a, :].bitcast(U8).bitcast(FP4X4),
-                    rhs_scale=w_s[m][:].bitcast(U8)[:, a, HALF * b : HALF * (b + 1)],
+                    rhs=w_early[m][:, a, :].bitcast(U8).bitcast(FP4X4),
+                    rhs_scale=w_s[m][:].bitcast(U8)[:, a, :HALF],
                     start=(a == 0),
                     stop=(a == 1),
                 )
+            return acc[:].rearrange("j (p u e) -> j u p e", u=2, e=2)
 
-        def gate_half(jt, b):
-            ga = psum.tile([P, HALF], F32, name="ga", tag="ga", bufs=2)
-            product(0, jt, b, ga)
-            th[jt, b] = sb([P, 2, P, 2], F32, f"th{jt}{b}")
-            nc.scalar.activation(out=th[jt, b][:], in_=ga[:].rearrange("j (p u e) -> j u p e", u=2, e=2), func=TANH, bias=zero[:])
+        def early_gate(jt):
+            ga = early_product(0, jt)
+            th[jt, 0] = sb([P, 2, P, 2], F32, f"th{jt}0")
+            nc.scalar.activation(out=th[jt, 0][:], in_=ga, func=TANH, bias=zero[:])
 
-        def up_half(jt, b):
-            ub = psum.tile([P, HALF], F32, name="ub", tag="ub", bufs=3)
-            product(1, jt, b, ub)
-            nc.vector.tensor_tensor(
-                out=h_rows[jt][:, b, :].rearrange("j (u p e) -> j u p e", u=2, e=2),
-                in0=ub[:].rearrange("j (p u e) -> j u p e", u=2, e=2),
-                in1=th[jt, b][:],
-                op=MULT,
-            )
+        def early_up(jt):
+            ub = early_product(1, jt)
+            nc.vector.tensor_tensor(out=h_rows[jt][:].rearrange("j (u p e) -> j u p e", u=2, e=2), in0=ub, in1=th[jt, 0][:], op=MULT)
 
-        def unit(jt, b):
-            gate_half(jt, b)
-            up_half(jt, b)
+        def late_product(m, jt):
+            acc = bank([P, 4, P])
+            for t in range(4):
+                for a in range(2):
+                    nc.tensor.matmul_mx(
+                        out=acc[:, t, :],
+                        lhsT=dealt_w[m][:, a, t, :].bitcast(U8).bitcast(FP4X4),
+                        lhsT_scale=dealt_s[m][:, a, t, :].bitcast(U8),
+                        rhs=stat_w[jt][:, a, :].bitcast(FP4X4),
+                        rhs_scale=stat_s[jt][:, a, :],
+                        start=(a == 0),
+                        stop=(a == 1),
+                    )
+            return acc[:].rearrange("p t j -> p j t")
 
-        h_cols = sb([P, 2, J, 4], BF16, "h_cols")
-        h_codes = sb([P, 2, J], U32, "h_codes")
-        h_scales = sb([P, 2, J], U8, "h_scales")
+        def late_unit(jt):
+            ga = late_product(0, jt)
+            th[jt, 1] = sb([P, P, 4], F32, f"th{jt}1")
+            nc.scalar.activation(out=th[jt, 1][:], in_=ga, func=TANH, bias=zero[:])
+            ub = late_product(1, jt)
+            nc.vector.tensor_tensor(out=h_cols[1][:, P * jt : P * (jt + 1), :], in0=ub, in1=th[jt, 1][:], op=MULT)
 
-        def turn(b, jt0, jt1):
-            turned = psum.tile([P, 2, 2, P], F32, name="turned", tag="turned", bufs=2)
+        def turn(jt0, jt1):
+            turned = bank([P, 2, 2, P])
             for jt in range(jt0, jt1):
                 words = h_rows[jt][:].bitcast(F32)
                 for u in range(2):
-                    nc.tensor.transpose(turned[:, jt - jt0, u, :], words[:, b, P * u : P * (u + 1)], ident[:])
+                    nc.tensor.transpose(turned[:, jt - jt0, u, :], words[:, P * u : P * (u + 1)], ident[:])
             nc.scalar.copy(
-                out=h_cols[:].bitcast(F32)[:, b, P * jt0 : P * jt1, :].rearrange("p (i j) u -> p i j u", j=P),
-                in_=turned[:, : jt1 - jt0].rearrange("p i u j -> p i j u"),
+                out=h_cols[0][:].bitcast(F32)[:, P * jt0 : P * jt1, :].rearrange("p (i j) u -> p i j u", j=P),
+                in_=turned[:].rearrange("p i u j -> p i j u"),
             )
 
         def quantise_h(b, j0, j1):
             nc.vector.quantize_mx(
                 out=h_codes[:, b, j0:j1].bitcast(FP8X4),
                 scales=h_scales[:, b, j0:j1],
-                in_=h_cols[:, b, j0:j1, :].rearrange("p j t -> p (j t)"),
+                in_=h_cols[b][:, j0:j1, :].rearrange("p j t -> p (j t)"),
             )
 
         wd_codes = sb([P, 2, N], U32, "wd_codes")
@@ -180,7 +208,7 @@ def tile_list_gmlpt_tanh_gate_kernel(
         out_view = out.rearrange("(c p) j -> p c j", c=2)
 
         def second_layer(j0, j1):
-            y = psum.tile([P, 2, j1 - j0], F32, name="y", tag="y", bufs=1)
+            y = bank([P, 2, j1 - j0])
             for c in range(2):
                 for b in range(2):
                     nc.tensor.matmul_mx(
@@ -199,33 +227,34 @@ def tile_list_gmlpt_tanh_gate_kernel(
         pick_scales(0, 256, sb([P, 2, 256], U8, "picked_s0"))
         pick_words(0, 128, sb([P, P], U32, "picked_w0"))
         pick_words(128, 256, at(256, [P, P], U32, "picked_w1"))
-        gate_half(0, 0)
-        gate_half(1, 0)
+        early_gate(0)
+        early_gate(1)
         pick_scales(256, 512, at(0, [P, 2, 256], U8, "picked_s1"))
         pick_words(256, 512, at(512, [P, 2 * P], U32, "picked_w2"))
-        gate_half(2, 0)
-        gate_half(3, 0)
+        early_gate(2)
+        early_gate(3)
+        deal(0)
         pick_gate(0, 0, 512)
+        deal(1)
+        early_up(0)
+        early_up(1)
         pick_gate(1, 0, 512)
-        for jt in range(4):
-            up_half(jt, 0)
+        early_up(2)
+        early_up(3)
+        late_unit(0)
         prepare_wd(0, 0, None)
         prepare_wd(0, 1, None)
-        unit(0, 1)
+        turn(0, 2)
+        late_unit(1)
         prepare_wd(1, 0, None)
-        turn(0, 0, 2)
-        turn(0, 2, 4)
-        unit(1, 1)
+        prepare_wd(1, 1, None)
+        turn(2, 4)
         quantise_h(0, 0, 256)
-        quantise_h(0, 256, 512)
-        unit(2, 1)
-        prepare_wd(1, 1, "th11")
-        turn(1, 0, 2)
-        unit(3, 1)
+        late_unit(2)
         quantise_h(1, 0, 256)
-        turn(1, 2, 3)
         second_layer(0, 256)
-        turn(1, 3, 4)
+        quantise_h(0, 256, 512)
+        late_unit(3)
         quantise_h(1, 256, 384)
         second_layer(256, 384)
         quantise_h(1, 384, 512)

@@ -96,6 +96,15 @@ def tile_list_gmlpt_tanh_gate_kernel(
             for jt in range(j0 // P, j1 // P):
                 stat_s[jt] = picked[:, :, P * jt - j0 : P * (jt + 1) - j0]
 
+        def pick_tile(jt, words, scales):
+            j0, j1 = P * jt, P * (jt + 1)
+            parted = sb([P, 2, 2 * P], U8, f"parted{j0}")
+            nc.vector.tensor_copy(out=words[:], in_=tab_w[:].bitcast(U32).indirect(lst(j0, j1)))
+            nc.vector.tensor_copy(out=scales[:, 0, :], in_=tab_s8[:, 0, :].indirect(lst(j0, j1)))
+            nc.vector.tensor_copy(out=parted[:].bitcast(U16), in_=words[:].bitcast(U16).rearrange("p (j d) -> p d j", d=2))
+            nc.vector.tensor_copy(out=scales[:, 1, :], in_=tab_s8[:, 1, :].indirect(lst(j0, j1)))
+            stat_w[jt], stat_s[jt] = parted[:], scales[:]
+
         def pick_words(j0, j1, picked):
             parted = sb([P, 2, 2 * (j1 - j0)], U8, f"parted{j0}")
             nc.vector.tensor_copy(out=picked[:], in_=tab_w[:].bitcast(U32).indirect(lst(j0, j1)))
@@ -207,31 +216,49 @@ def tile_list_gmlpt_tanh_gate_kernel(
 
         out_view = out.rearrange("(c p) j -> p c j", c=2)
 
+        def down_pass(y, c, b, j0, j1):
+            nc.tensor.matmul_mx(
+                out=y,
+                lhsT=wd_codes[:, b, P * c : P * (c + 1)].bitcast(FP8X4),
+                lhsT_scale=wd_scales[:, b, P * c : P * (c + 1)],
+                rhs=h_codes[:, b, j0:j1].bitcast(FP8X4),
+                rhs_scale=h_scales[:, b, j0:j1],
+                start=(b == 0),
+                stop=(b == 1),
+            )
+
         def second_layer(j0, j1):
             y = bank([P, 2, j1 - j0])
             for c in range(2):
                 for b in range(2):
-                    nc.tensor.matmul_mx(
-                        out=y[:, c, :],
-                        lhsT=wd_codes[:, b, P * c : P * (c + 1)].bitcast(FP8X4),
-                        lhsT_scale=wd_scales[:, b, P * c : P * (c + 1)],
-                        rhs=h_codes[:, b, j0:j1].bitcast(FP8X4),
-                        rhs_scale=h_scales[:, b, j0:j1],
-                        start=(b == 0),
-                        stop=(b == 1),
-                    )
+                    down_pass(y[:, c, :], c, b, j0, j1)
             res = sb([P, 2, j1 - j0], F32, f"res{j0}")
             nc.vector.tensor_tensor(out=res[:], in0=y[:], in1=picked_g[:, :, j0:j1], op=MULT)
             nc.sync.dma_start(out=out_view[:, :, j0:j1], in_=res[:])
 
-        pick_scales(0, 256, sb([P, 2, 256], U8, "picked_s0"))
+        def warm_up(passes):
+            acc = bank([P, 2 * P])
+            for i in range(passes):
+                nc.tensor.matmul_mx(
+                    out=acc[:],
+                    lhsT=wg_early[:, 0, : P // 2].bitcast(U8).bitcast(FP4X4),
+                    lhsT_scale=first_s[:, 0, :P],
+                    rhs=wg_early[:, 0, :P].bitcast(U8).bitcast(FP4X4),
+                    rhs_scale=first_s[:, 0, :],
+                    start=(i == 0),
+                    stop=(i == passes - 1),
+                )
+
+        first_s = sb([P, 2, 256], U8, "picked_s0")
+        pick_scales(0, 256, first_s)
+        warm_up(5)
         pick_words(0, 128, sb([P, P], U32, "picked_w0"))
         pick_words(128, 256, at(256, [P, P], U32, "picked_w1"))
         early_gate(0)
         early_gate(1)
-        pick_scales(256, 512, at(0, [P, 2, 256], U8, "picked_s1"))
-        pick_words(256, 512, at(512, [P, 2 * P], U32, "picked_w2"))
+        pick_tile(2, at(640, [P, P], U32, "picked_w2"), at(128, [P, 2, P], U8, "picked_s2"))
         early_gate(2)
+        pick_tile(3, sb([P, P], U32, "picked_w3", "picked_w0"), at(384, [P, 2, P], U8, "picked_s3"))
         early_gate(3)
         deal(0)
         pick_gate(0, 0, 512)
@@ -251,11 +278,18 @@ def tile_list_gmlpt_tanh_gate_kernel(
         turn(2, 4)
         quantise_h(0, 0, 256)
         late_unit(2)
-        quantise_h(1, 0, 256)
-        second_layer(0, 256)
-        quantise_h(0, 256, 512)
         late_unit(3)
+        quantise_h(1, 0, 256)
+        quantise_h(0, 256, 512)
+        second_layer(0, 256)
+        last_y = [bank([P, P]) for c in range(2)]
+        for c in range(2):
+            down_pass(last_y[c][:], c, 0, 384, 512)
         quantise_h(1, 256, 384)
         second_layer(256, 384)
         quantise_h(1, 384, 512)
-        second_layer(384, 512)
+        res = sb([P, 2, P], F32, "res_last")
+        for c in range(2):
+            down_pass(last_y[c][:], c, 1, 384, 512)
+            nc.vector.tensor_tensor(out=res[:, c, :], in0=last_y[c][:], in1=picked_g[:, c, 384:512], op=MULT)
+            nc.sync.dma_start(out=out_view[:, c, 384:512], in_=res[:, c, :])

@@ -124,11 +124,11 @@ def tile_list_gmlpt_tanh_gate_kernel(
             return psum.tile(shape, F32, name="bank", tag="bank", bufs=8)
 
         def deal(m):
-            nc.vector.tensor_copy(
+            nc.gpsimd.tensor_copy(
                 out=dealt_s[m][:].rearrange("p a t (q e) -> p a t q e", e=2),
                 in_=w_s[m][:, :, HALF // 4 :].rearrange("p a (q t e) -> p a t q e", t=4, e=2),
             )
-            nc.vector.tensor_copy(
+            nc.gpsimd.tensor_copy(
                 out=dealt_w[m][:].rearrange("p a t (q e) -> p a t q e", e=4),
                 in_=w_late[m][:].rearrange("p a (q t e) -> p a t q e", t=4, e=4),
             )

@@ -72,15 +72,15 @@ def tile_list_gmlpt_tanh_gate_kernel(
         nc.sync.dma_start(out=tab_w[:], in_=tab_words[0].rearrange("p t d -> p (t d)").bitcast(I32))
         load_scales(w_s[0], wg_scales)
         load_words(wu_early[:], 1, 0)
+        nc.sync.dma_start(out=gate[:, 0, :], in_=gT[:P, :])
+        nc.sync.dma_start(out=wd_raw[0][:], in_=wd[:HALF].rearrange("(p t) n -> p t n", t=4))
+        load_scales(w_s[1], wu_scales)
         for m in range(2):
             load_words(w_late[m][:], m, 1)
-        nc.sync.dma_start(out=gate[:, 0, :], in_=gT[:P, :])
-        load_scales(w_s[1], wu_scales)
-        nc.sync.dma_start(out=gate[:, 1, :], in_=gT[P:, :])
-        nc.sync.dma_start(out=wd_raw[0][:], in_=wd[:HALF].rearrange("(p t) n -> p t n", t=4))
         late_rows = wd[HALF:].rearrange("(q t i) n -> t q i n", t=4, i=8)
         for t in range(4):
             nc.sync.dma_start(out=wd_raw[1][:, t, :], in_=late_rows[t])
+        nc.sync.dma_start(out=gate[:, 1, :], in_=gT[P:, :])
         w_early = [wg_early, wu_early]
 
         tab_s8 = tab_s[:].bitcast(U8)
@@ -169,14 +169,23 @@ def tile_list_gmlpt_tanh_gate_kernel(
                         start=(a == 0),
                         stop=(a == 1),
                     )
-            return acc[:].rearrange("p t j -> p j t")
+            return acc
 
-        def late_unit(jt):
+        ub_late = {}
+
+        def late_products(jt):
             ga = late_product(0, jt)
-            th[jt, 1] = sb([P, P, 4], F32, f"th{jt}1")
-            nc.scalar.activation(out=th[jt, 1][:], in_=ga, func=TANH, bias=zero[:])
-            ub = late_product(1, jt)
-            nc.vector.tensor_tensor(out=h_cols[1][:, P * jt : P * (jt + 1), :], in0=ub, in1=th[jt, 1][:], op=MULT)
+            th[jt, 1] = sb([P, 4, P], F32, f"th{jt}1")
+            nc.scalar.activation(out=th[jt, 1][:], in_=ga[:], func=TANH, bias=zero[:])
+            ub_late[jt] = late_product(1, jt)
+
+        def late_mult(jt):
+            nc.vector.tensor_tensor(
+                out=h_cols[1][:, P * jt : P * (jt + 1), :].rearrange("p (c i) t -> p c t i", i=2),
+                in0=ub_late[jt][:].rearrange("p t (c i) -> p c t i", i=2),
+                in1=th[jt, 1][:].rearrange("p t (c i) -> p c t i", i=2),
+                op=MULT,
+            )
 
         def turn(jt0, jt1):
             turned = bank([P, 2, 2, P])
@@ -185,8 +194,8 @@ def tile_list_gmlpt_tanh_gate_kernel(
                 for u in range(2):
                     nc.tensor.transpose(turned[:, jt - jt0, u, :], words[:, P * u : P * (u + 1)], ident[:])
             nc.scalar.copy(
-                out=h_cols[0][:].bitcast(F32)[:, P * jt0 : P * jt1, :].rearrange("p (i j) u -> p i j u", j=P),
-                in_=turned[:].rearrange("p i u j -> p i j u"),
+                out=h_cols[0][:].bitcast(F32)[:, P * jt0 : P * jt1, :].rearrange("p (i c k) u -> p i c u k", i=2, k=2),
+                in_=turned[:].rearrange("p i u (c k) -> p i c u k", k=2),
             )
 
         def quantise_h(b, j0, j1):
@@ -202,7 +211,9 @@ def tile_list_gmlpt_tanh_gate_kernel(
         def prepare_wd(b, c, tag):
             cols = slice(P * c, P * (c + 1))
             wd_bf = sb([P, P, 4], BF16, f"wd_bf{b}{c}", tag)
-            nc.scalar.copy(out=wd_bf[:], in_=wd_raw[b][:, :, cols].rearrange("p t n -> p n t"))
+            nc.scalar.copy(
+                out=wd_bf[:].rearrange("p (c i) t -> p c t i", i=2), in_=wd_raw[b][:, :, cols].rearrange("p t (c i) -> p c t i", i=2)
+            )
             nc.vector.quantize_mx(
                 out=wd_codes[:, b, cols].bitcast(FP8X4),
                 scales=wd_scales[:, b, cols],
@@ -227,12 +238,12 @@ def tile_list_gmlpt_tanh_gate_kernel(
                 stop=(b == 1),
             )
 
-        def second_layer(j0, j1):
+        def second_layer(j0, j1, tag):
             y = bank([P, 2, j1 - j0])
             for c in range(2):
                 for b in range(2):
                     down_pass(y[:, c, :], c, b, j0, j1)
-            res = sb([P, 2, j1 - j0], F32, f"res{j0}")
+            res = sb([P, 2, j1 - j0], F32, f"res{j0}", tag)
             nc.vector.tensor_tensor(out=res[:], in0=y[:], in1=picked_g[:, :, j0:j1], op=MULT)
             nc.sync.dma_start(out=out_view[:, :, j0:j1], in_=res[:])
 
@@ -260,34 +271,36 @@ def tile_list_gmlpt_tanh_gate_kernel(
         early_gate(2)
         pick_tile(3, sb([P, P], U32, "picked_w3", "picked_w0"), at(384, [P, 2, P], U8, "picked_s3"))
         early_gate(3)
-        deal(0)
         pick_gate(0, 0, 512)
+        for jt in range(4):
+            early_up(jt)
+        deal(0)
         deal(1)
-        early_up(0)
-        early_up(1)
-        pick_gate(1, 0, 512)
-        early_up(2)
-        early_up(3)
-        late_unit(0)
         prepare_wd(0, 0, None)
         prepare_wd(0, 1, None)
+        late_products(0)
         turn(0, 2)
-        late_unit(1)
+        late_mult(0)
+        late_products(1)
+        turn(2, 4)
         prepare_wd(1, 0, None)
         prepare_wd(1, 1, None)
-        turn(2, 4)
+        pick_gate(1, 0, 512)
         quantise_h(0, 0, 256)
-        late_unit(2)
-        late_unit(3)
-        quantise_h(1, 0, 256)
+        late_mult(1)
+        late_products(2)
         quantise_h(0, 256, 512)
-        second_layer(0, 256)
+        quantise_h(1, 0, 256)
+        late_mult(2)
+        late_products(3)
+        quantise_h(1, 256, 384)
+        late_mult(3)
+        quantise_h(1, 384, 512)
+        second_layer(0, 256, "h_cols1")
         last_y = [bank([P, P]) for c in range(2)]
         for c in range(2):
             down_pass(last_y[c][:], c, 0, 384, 512)
-        quantise_h(1, 256, 384)
-        second_layer(256, 384)
-        quantise_h(1, 384, 512)
+        second_layer(256, 384, None)
         res = sb([P, 2, P], F32, "res_last")
         for c in range(2):
             down_pass(last_y[c][:], c, 1, 384, 512)

@@ -73,14 +73,14 @@ def tile_list_gmlpt_tanh_gate_kernel(
         load_scales(w_s[0], wg_scales)
         load_words(wu_early[:], 1, 0)
         nc.sync.dma_start(out=gate[:, 0, :], in_=gT[:P, :])
-        nc.sync.dma_start(out=wd_raw[0][:], in_=wd[:HALF].rearrange("(p t) n -> p t n", t=4))
         load_scales(w_s[1], wu_scales)
-        for m in range(2):
-            load_words(w_late[m][:], m, 1)
+        load_words(w_late[0][:], 0, 1)
+        load_words(w_late[1][:], 1, 1)
+        nc.sync.dma_start(out=wd_raw[0][:], in_=wd[:HALF].rearrange("(p t) n -> p t n", t=4))
+        nc.sync.dma_start(out=gate[:, 1, :], in_=gT[P:, :])
         late_rows = wd[HALF:].rearrange("(q t i) n -> t q i n", t=4, i=8)
         for t in range(4):
             nc.sync.dma_start(out=wd_raw[1][:, t, :], in_=late_rows[t])
-        nc.sync.dma_start(out=gate[:, 1, :], in_=gT[P:, :])
         w_early = [wg_early, wu_early]
 
         tab_s8 = tab_s[:].bitcast(U8)
@@ -173,11 +173,17 @@ def tile_list_gmlpt_tanh_gate_kernel(
 
         ub_late = {}
 
-        def late_products(jt):
+        def late_gate(jt):
             ga = late_product(0, jt)
             th[jt, 1] = sb([P, 4, P], F32, f"th{jt}1")
             nc.scalar.activation(out=th[jt, 1][:], in_=ga[:], func=TANH, bias=zero[:])
+
+        def late_up(jt):
             ub_late[jt] = late_product(1, jt)
+
+        def late_products(jt):
+            late_gate(jt)
+            late_up(jt)
 
         def late_mult(jt):
             nc.vector.tensor_tensor(
@@ -205,15 +211,12 @@ def tile_list_gmlpt_tanh_gate_kernel(
                 in_=h_cols[b][:, j0:j1, :].rearrange("p j t -> p (j t)"),
             )
 
-        wd_codes = sb([P, 2, N], U32, "wd_codes")
-        wd_scales = sb([P, 2, N], U8, "wd_scales")
 
         def prepare_wd(b, c, tag):
             cols = slice(P * c, P * (c + 1))
             wd_bf = sb([P, P, 4], BF16, f"wd_bf{b}{c}", tag)
-            nc.scalar.copy(
-                out=wd_bf[:].rearrange("p (c i) t -> p c t i", i=2), in_=wd_raw[b][:, :, cols].rearrange("p t (c i) -> p c t i", i=2)
-            )
+            copy = nc.scalar.copy if b == 0 else nc.gpsimd.tensor_copy
+            copy(out=wd_bf[:].rearrange("p (c i) t -> p c t i", i=2), in_=wd_raw[b][:, :, cols].rearrange("p t (c i) -> p c t i", i=2))
             nc.vector.quantize_mx(
                 out=wd_codes[:, b, cols].bitcast(FP8X4),
                 scales=wd_scales[:, b, cols],
@@ -263,19 +266,21 @@ def tile_list_gmlpt_tanh_gate_kernel(
         first_s = sb([P, 2, 256], U8, "picked_s0")
         pick_scales(0, 256, first_s)
         warm_up(5)
-        pick_words(0, 128, sb([P, P], U32, "picked_w0"))
-        pick_words(128, 256, at(256, [P, P], U32, "picked_w1"))
+        pick_words(0, 128, at(256, [P, P], U32, "picked_w0"))
+        pick_words(128, 256, sb([P, P], U32, "picked_w1"))
         early_gate(0)
         early_gate(1)
         pick_tile(2, at(640, [P, P], U32, "picked_w2"), at(128, [P, 2, P], U8, "picked_s2"))
         early_gate(2)
-        pick_tile(3, sb([P, P], U32, "picked_w3", "picked_w0"), at(384, [P, 2, P], U8, "picked_s3"))
+        pick_tile(3, sb([P, P], U32, "picked_w3", "picked_w1"), at(896, [P, 2, P], U8, "picked_s3"))
         early_gate(3)
         pick_gate(0, 0, 512)
         for jt in range(4):
             early_up(jt)
         deal(0)
         deal(1)
+        wd_codes = sb([P, 2, N], U32, "wd_codes", "th10")
+        wd_scales = sb([P, 2, N], U8, "wd_scales")
         prepare_wd(0, 0, None)
         prepare_wd(0, 1, None)
         late_products(0)
@@ -288,13 +293,15 @@ def tile_list_gmlpt_tanh_gate_kernel(
         pick_gate(1, 0, 512)
         quantise_h(0, 0, 256)
         late_mult(1)
-        late_products(2)
+        late_gate(2)
+        late_gate(3)
+        late_up(2)
+        late_up(3)
         quantise_h(0, 256, 512)
         quantise_h(1, 0, 256)
         late_mult(2)
-        late_products(3)
-        quantise_h(1, 256, 384)
         late_mult(3)
+        quantise_h(1, 256, 384)
         quantise_h(1, 384, 512)
         second_layer(0, 256, "h_cols1")
         last_y = [bank([P, P]) for c in range(2)]

@@ -70,14 +70,14 @@ def tile_list_gmlpt_tanh_gate_kernel(
         load_words(wg_early[:], 0, 0)
         load_scales(tab_s, tab_scales)
         nc.sync.dma_start(out=tab_w[:], in_=tab_words[0].rearrange("p t d -> p (t d)").bitcast(I32))
+        load_words(w_late[0][:], 0, 1)
         load_scales(w_s[0], wg_scales)
         load_words(wu_early[:], 1, 0)
         nc.sync.dma_start(out=gate[:, 0, :], in_=gT[:P, :])
+        nc.sync.dma_start(out=gate[:, 1, :], in_=gT[P:, :])
         load_scales(w_s[1], wu_scales)
-        load_words(w_late[0][:], 0, 1)
         load_words(w_late[1][:], 1, 1)
         nc.sync.dma_start(out=wd_raw[0][:], in_=wd[:HALF].rearrange("(p t) n -> p t n", t=4))
-        nc.sync.dma_start(out=gate[:, 1, :], in_=gT[P:, :])
         late_rows = wd[HALF:].rearrange("(q t i) n -> t q i n", t=4, i=8)
         for t in range(4):
             nc.sync.dma_start(out=wd_raw[1][:, t, :], in_=late_rows[t])
@@ -90,27 +90,18 @@ def tile_list_gmlpt_tanh_gate_kernel(
 
         stat_w, stat_s = {}, {}
 
-        def pick_scales(j0, j1, picked):
+        def pick_scales(picked, j0, j1):
             for a in range(2):
-                nc.vector.tensor_copy(out=picked[:, a, :], in_=tab_s8[:, a, :].indirect(lst(j0, j1)))
+                nc.vector.tensor_copy(out=picked[:, a, j0 % 256 : j0 % 256 + j1 - j0], in_=tab_s8[:, a, :].indirect(lst(j0, j1)))
             for jt in range(j0 // P, j1 // P):
-                stat_s[jt] = picked[:, :, P * jt - j0 : P * (jt + 1) - j0]
+                stat_s[jt] = picked[:, :, P * (jt % 2) : P * (jt % 2 + 1)]
 
-        def pick_tile(jt, words, scales):
-            j0, j1 = P * jt, P * (jt + 1)
-            parted = sb([P, 2, 2 * P], U8, f"parted{j0}")
-            nc.vector.tensor_copy(out=words[:], in_=tab_w[:].bitcast(U32).indirect(lst(j0, j1)))
-            nc.vector.tensor_copy(out=scales[:, 0, :], in_=tab_s8[:, 0, :].indirect(lst(j0, j1)))
-            nc.vector.tensor_copy(out=parted[:].bitcast(U16), in_=words[:].bitcast(U16).rearrange("p (j d) -> p d j", d=2))
-            nc.vector.tensor_copy(out=scales[:, 1, :], in_=tab_s8[:, 1, :].indirect(lst(j0, j1)))
-            stat_w[jt], stat_s[jt] = parted[:], scales[:]
+        parted = [sb([P, 2, 4 * P], U8, f"parted{i}") for i in range(2)]
 
-        def pick_words(j0, j1, picked):
-            parted = sb([P, 2, 2 * (j1 - j0)], U8, f"parted{j0}")
-            nc.vector.tensor_copy(out=picked[:], in_=tab_w[:].bitcast(U32).indirect(lst(j0, j1)))
-            nc.vector.tensor_copy(out=parted[:].bitcast(U16), in_=picked[:].bitcast(U16).rearrange("p (j d) -> p d j", d=2))
-            for jt in range(j0 // P, j1 // P):
-                stat_w[jt] = parted[:, :, 2 * (P * jt - j0) : 2 * (P * (jt + 1) - j0)]
+        def pick_words(jt, words):
+            stat_w[jt] = parted[jt // 2][:, :, 2 * P * (jt % 2) : 2 * P * (jt % 2 + 1)]
+            nc.vector.tensor_copy(out=words[:], in_=tab_w[:].bitcast(U32).indirect(lst(P * jt, P * (jt + 1))))
+            nc.vector.tensor_copy(out=stat_w[jt].bitcast(U16), in_=words[:].bitcast(U16).rearrange("p (j d) -> p d j", d=2))
 
         h_rows = [sb([P, HALF], BF16, f"h_rows{jt}") for jt in range(4)]
         h_cols = [sb([P, J, 4], BF16, f"h_cols{b}") for b in range(2)]
@@ -120,8 +111,10 @@ def tile_list_gmlpt_tanh_gate_kernel(
         dealt_s = [sb([P, 2, 4, P // 4], I32, f"dealt_s{m}") for m in range(2)]
         th = {}
 
-        def bank(shape):
-            return psum.tile(shape, F32, name="bank", tag="bank", bufs=8)
+        def bank(shape, own=None):
+            if own is not None:
+                return psum.tile(shape, F32, name="own_bank", tag=f"own_bank{own}", bufs=1)
+            return psum.tile(shape, F32, name="bank", tag="bank", bufs=6)
 
         def deal(m):
             nc.gpsimd.tensor_copy(
@@ -134,7 +127,7 @@ def tile_list_gmlpt_tanh_gate_kernel(
             )
 
         def early_product(m, jt):
-            acc = bank([P, HALF])
+            acc = bank([P, HALF], jt if m == 1 and jt < 2 else None)
             for a in range(2):
                 nc.tensor.matmul_mx(
                     out=acc[:],
@@ -156,40 +149,38 @@ def tile_list_gmlpt_tanh_gate_kernel(
             ub = early_product(1, jt)
             nc.vector.tensor_tensor(out=h_rows[jt][:].rearrange("j (u p e) -> j u p e", u=2, e=2), in0=ub, in1=th[jt, 0][:], op=MULT)
 
-        def late_product(m, jt):
-            acc = bank([P, 4, P])
-            for t in range(4):
-                for a in range(2):
-                    nc.tensor.matmul_mx(
-                        out=acc[:, t, :],
-                        lhsT=dealt_w[m][:, a, t, :].bitcast(U8).bitcast(FP4X4),
-                        lhsT_scale=dealt_s[m][:, a, t, :].bitcast(U8),
-                        rhs=stat_w[jt][:, a, :].bitcast(FP4X4),
-                        rhs_scale=stat_s[jt][:, a, :],
-                        start=(a == 0),
-                        stop=(a == 1),
-                    )
-            return acc
+        def late_pass(out_ap, m, t, words, scales):
+            for a in range(2):
+                nc.tensor.matmul_mx(
+                    out=out_ap,
+                    lhsT=dealt_w[m][:, a, t, :].bitcast(U8).bitcast(FP4X4),
+                    lhsT_scale=dealt_s[m][:, a, t, :].bitcast(U8),
+                    rhs=words[:, a, :].bitcast(FP4X4),
+                    rhs_scale=scales[:, a, :],
+                    start=(a == 0),
+                    stop=(a == 1),
+                )
+
+        def late_gate(i):
+            th[i, 1] = sb([P, 4, 2 * P], F32, f"th{i}1")
+            for u in range(2):
+                ga = bank([P, 2, 2 * P], u if i == 1 else None)
+                for e in range(2):
+                    late_pass(ga[:, e, :], 0, 2 * u + e, parted[i][:], pair_s[i][:])
+                nc.scalar.activation(out=th[i, 1][:, 2 * u : 2 * u + 2, :], in_=ga[:], func=TANH, bias=zero[:])
 
         ub_late = {}
 
-        def late_gate(jt):
-            ga = late_product(0, jt)
-            th[jt, 1] = sb([P, 4, P], F32, f"th{jt}1")
-            nc.scalar.activation(out=th[jt, 1][:], in_=ga[:], func=TANH, bias=zero[:])
-
         def late_up(jt):
-            ub_late[jt] = late_product(1, jt)
-
-        def late_products(jt):
-            late_gate(jt)
-            late_up(jt)
+            ub_late[jt] = bank([P, 4, P])
+            for t in range(4):
+                late_pass(ub_late[jt][:, t, :], 1, t, stat_w[jt], stat_s[jt])
 
         def late_mult(jt):
             nc.vector.tensor_tensor(
                 out=h_cols[1][:, P * jt : P * (jt + 1), :].rearrange("p (c i) t -> p c t i", i=2),
                 in0=ub_late[jt][:].rearrange("p t (c i) -> p c t i", i=2),
-                in1=th[jt, 1][:].rearrange("p t (c i) -> p c t i", i=2),
+                in1=th[jt // 2, 1][:, :, P * (jt % 2) : P * (jt % 2 + 1)].rearrange("p t (c i) -> p c t i", i=2),
                 op=MULT,
             )
 
@@ -256,45 +247,47 @@ def tile_list_gmlpt_tanh_gate_kernel(
                 nc.tensor.matmul_mx(
                     out=acc[:],
                     lhsT=wg_early[:, 0, : P // 2].bitcast(U8).bitcast(FP4X4),
-                    lhsT_scale=first_s[:, 0, :P],
+                    lhsT_scale=pair_s[0][:, 0, :P],
                     rhs=wg_early[:, 0, :P].bitcast(U8).bitcast(FP4X4),
-                    rhs_scale=first_s[:, 0, :],
+                    rhs_scale=pair_s[0][:, 0, :],
                     start=(i == 0),
                     stop=(i == passes - 1),
                 )
 
-        first_s = sb([P, 2, 256], U8, "picked_s0")
-        pick_scales(0, 256, first_s)
+        pair_s = [sb([P, 2, 256], U8, "picked_s0")]
+        pick_scales(pair_s[0], 0, 256)
         warm_up(5)
-        pick_words(0, 128, at(256, [P, P], U32, "picked_w0"))
-        pick_words(128, 256, sb([P, P], U32, "picked_w1"))
+        pick_words(0, at(256, [P, P], U32, "picked_w0"))
+        pick_words(1, sb([P, P], U32, "picked_w1"))
         early_gate(0)
         early_gate(1)
-        pick_tile(2, at(640, [P, P], U32, "picked_w2"), at(128, [P, 2, P], U8, "picked_s2"))
+        deal(0)
+        late_gate(0)
+        pick_words(2, at(640, [P, P], U32, "picked_w2"))
+        pair_s.append(at(0, [P, 2, 256], U8, "picked_s1"))
+        pick_scales(pair_s[1], 256, 512)
         early_gate(2)
-        pick_tile(3, sb([P, P], U32, "picked_w3", "picked_w1"), at(896, [P, 2, P], U8, "picked_s3"))
+        pick_words(3, sb([P, P], U32, "picked_w3", "picked_w1"))
         early_gate(3)
         pick_gate(0, 0, 512)
+        pick_gate(1, 0, 512)
         for jt in range(4):
             early_up(jt)
-        deal(0)
         deal(1)
         wd_codes = sb([P, 2, N], U32, "wd_codes", "th10")
         wd_scales = sb([P, 2, N], U8, "wd_scales")
         prepare_wd(0, 0, None)
         prepare_wd(0, 1, None)
-        late_products(0)
+        late_up(0)
+        late_up(1)
         turn(0, 2)
-        late_mult(0)
-        late_products(1)
         turn(2, 4)
+        late_mult(0)
         prepare_wd(1, 0, None)
         prepare_wd(1, 1, None)
-        pick_gate(1, 0, 512)
-        quantise_h(0, 0, 256)
         late_mult(1)
-        late_gate(2)
-        late_gate(3)
+        quantise_h(0, 0, 256)
+        late_gate(1)
         late_up(2)
         late_up(3)
         quantise_h(0, 256, 512)
@@ -303,7 +296,18 @@ def tile_list_gmlpt_tanh_gate_kernel(
         late_mult(3)
         quantise_h(1, 256, 384)
         quantise_h(1, 384, 512)
-        second_layer(0, 256, "h_cols1")
+        y = bank([P, 2, 256])
+        for c in range(2):
+            for b in range(2):
+                down_pass(y[:, c, :], c, b, 0, 256)
+        y_sb = sb([P, 256], F32, "y_sb")
+        nc.scalar.copy(out=y_sb[:], in_=y[:, 1, :])
+        res_g = sb([P, 256], F32, "res_g")
+        nc.gpsimd.tensor_tensor(out=res_g[:], in0=y_sb[:], in1=picked_g[:, 1, :256], op=MULT)
+        nc.scalar.dma_start(out=out_view[:, 1, :256], in_=res_g[:])
+        res_v = sb([P, 256], F32, "res_v", "h_cols1")
+        nc.vector.tensor_tensor(out=res_v[:], in0=y[:, 0, :], in1=picked_g[:, 0, :256], op=MULT)
+        nc.sync.dma_start(out=out_view[:, 0, :256], in_=res_v[:])
         last_y = [bank([P, P]) for c in range(2)]
         for c in range(2):
             down_pass(last_y[c][:], c, 0, 384, 512)

@@ -206,7 +206,7 @@ def tile_list_gmlpt_tanh_gate_kernel(
         def prepare_wd(b, c, tag):
             cols = slice(P * c, P * (c + 1))
             wd_bf = sb([P, P, 4], BF16, f"wd_bf{b}{c}", tag)
-            copy = nc.scalar.copy if b == 0 else nc.gpsimd.tensor_copy
+            copy = nc.scalar.copy if c == 0 else nc.gpsimd.tensor_copy
             copy(out=wd_bf[:].rearrange("p (c i) t -> p c t i", i=2), in_=wd_raw[b][:, :, cols].rearrange("p t (c i) -> p c t i", i=2))
             nc.vector.quantize_mx(
                 out=wd_codes[:, b, cols].bitcast(FP8X4),
@@ -242,21 +242,21 @@ def tile_list_gmlpt_tanh_gate_kernel(
             nc.sync.dma_start(out=out_view[:, :, j0:j1], in_=res[:])
 
         def warm_up(passes):
-            acc = bank([P, 2 * P])
+            acc = bank([P, HALF])
             for i in range(passes):
                 nc.tensor.matmul_mx(
                     out=acc[:],
                     lhsT=wg_early[:, 0, : P // 2].bitcast(U8).bitcast(FP4X4),
-                    lhsT_scale=pair_s[0][:, 0, :P],
-                    rhs=wg_early[:, 0, :P].bitcast(U8).bitcast(FP4X4),
-                    rhs_scale=pair_s[0][:, 0, :],
+                    lhsT_scale=tab_s8[:, 0, :P],
+                    rhs=wg_early[:, 0, :].bitcast(U8).bitcast(FP4X4),
+                    rhs_scale=tab_s8[:, 0, :HALF],
                     start=(i == 0),
                     stop=(i == passes - 1),
                 )
 
         pair_s = [sb([P, 2, 256], U8, "picked_s0")]
         pick_scales(pair_s[0], 0, 256)
-        warm_up(5)
+        warm_up(3)
         pick_words(0, at(256, [P, P], U32, "picked_w0"))
         pick_words(1, sb([P, P], U32, "picked_w1"))
         early_gate(0)

@@ -1,7 +1,6 @@
 from contextlib import ExitStack
 
 import concourse.mybir as mybir
-from concourse.masks import make_identity
 
 K, R, N, T, J = 1024, 1024, 256, 1024, 512
 FLOPS = 2 * 2 * K * R * J + 2 * R * N * J
@@ -37,8 +36,8 @@ def tile_list_gmlpt_tanh_gate_kernel(
         tab_s = sb([P, 2, T // 4], I32, "tab_s")
         wg_early = sb([P, 2, HALF // 2], I32, "wg_early")
         ident = sb([P, P], F32, "ident")
-        zero_in = sb([P, 1], F32, "zero_in")
-        zero = sb([P, 1], F32, "zero")
+        zero_in = sb([P, P], F32, "zero_in")
+        zero = sb([P, P], F32, "zero")
 
         def at(offset, shape, dtype, name):
             return placed.tile(shape, dtype, name=name, offset=offset, align_bytes=64)
@@ -64,7 +63,9 @@ def tile_list_gmlpt_tanh_gate_kernel(
         nc.scalar.activation(out=zero[:], in_=zero_in[:], func=TANH)
         nc.vector.memset(w_s[0][:], 0)
         nc.gpsimd.memset(w_s[1][:], 0)
-        make_identity(nc, ident[:])
+        nc.gpsimd.affine_select(
+            out=ident[:], in_=zero[:], pattern=[[-1, P]], compare_op=mybir.AluOpType.not_equal, fill=1.0, base=0, channel_multiplier=1
+        )
 
         nc.sync.dma_start(offsets[:], offs)
         load_words(wg_early[:], 0, 0)
@@ -143,7 +144,7 @@ def tile_list_gmlpt_tanh_gate_kernel(
         def early_gate(jt):
             ga = early_product(0, jt)
             th[jt, 0] = sb([P, 2, P, 2], F32, f"th{jt}0")
-            nc.scalar.activation(out=th[jt, 0][:], in_=ga, func=TANH, bias=zero[:])
+            nc.scalar.activation(out=th[jt, 0][:], in_=ga, func=TANH)
 
         def early_up(jt):
             ub = early_product(1, jt)
@@ -167,7 +168,7 @@ def tile_list_gmlpt_tanh_gate_kernel(
                 ga = bank([P, 2, 2 * P], u if i == 1 else None)
                 for e in range(2):
                     late_pass(ga[:, e, :], 0, 2 * u + e, parted[i][:], pair_s[i][:])
-                nc.scalar.activation(out=th[i, 1][:, 2 * u : 2 * u + 2, :], in_=ga[:], func=TANH, bias=zero[:])
+                nc.scalar.activation(out=th[i, 1][:, 2 * u : 2 * u + 2, :], in_=ga[:], func=TANH)
 
         ub_late = {}
 
@@ -206,7 +207,7 @@ def tile_list_gmlpt_tanh_gate_kernel(
         def prepare_wd(b, c, tag):
             cols = slice(P * c, P * (c + 1))
             wd_bf = sb([P, P, 4], BF16, f"wd_bf{b}{c}", tag)
-            copy = nc.scalar.copy if c == 0 else nc.gpsimd.tensor_copy
+            copy = nc.scalar.copy if b == 0 else nc.gpsimd.tensor_copy
             copy(out=wd_bf[:].rearrange("p (c i) t -> p c t i", i=2), in_=wd_raw[b][:, :, cols].rearrange("p t (c i) -> p c t i", i=2))
             nc.vector.quantize_mx(
                 out=wd_codes[:, b, cols].bitcast(FP8X4),
@@ -305,7 +306,7 @@ def tile_list_gmlpt_tanh_gate_kernel(
         res_g = sb([P, 256], F32, "res_g")
         nc.gpsimd.tensor_tensor(out=res_g[:], in0=y_sb[:], in1=picked_g[:, 1, :256], op=MULT)
         nc.scalar.dma_start(out=out_view[:, 1, :256], in_=res_g[:])
-        res_v = sb([P, 256], F32, "res_v", "h_cols1")
+        res_v = sb([P, 256], F32, "res_v")
         nc.vector.tensor_tensor(out=res_v[:], in0=y[:, 0, :], in1=picked_g[:, 0, :256], op=MULT)
         nc.sync.dma_start(out=out_view[:, 0, :256], in_=res_v[:])
         last_y = [bank([P, P]) for c in range(2)]

@@ -207,8 +207,10 @@ def tile_list_gmlpt_tanh_gate_kernel(
         def prepare_wd(b, c, tag):
             cols = slice(P * c, P * (c + 1))
             wd_bf = sb([P, P, 4], BF16, f"wd_bf{b}{c}", tag)
-            copy = nc.scalar.copy if b == 0 else nc.gpsimd.tensor_copy
-            copy(out=wd_bf[:].rearrange("p (c i) t -> p c t i", i=2), in_=wd_raw[b][:, :, cols].rearrange("p t (c i) -> p c t i", i=2))
+            if b == 0:
+                nc.scalar.copy(out=wd_bf[:].rearrange("p (c i) t -> p c t i", i=2), in_=wd_raw[b][:, :, cols].rearrange("p t (c i) -> p c t i", i=2))
+            else:
+                nc.gpsimd.tensor_scalar(out=wd_bf[:], in0=wd_raw[b][:, :, cols].rearrange("p t n -> p n t"), scalar1=1.0, scalar2=0.0, op0=MULT, op1=mybir.AluOpType.add)
             nc.vector.quantize_mx(
                 out=wd_codes[:, b, cols].bitcast(FP8X4),
                 scales=wd_scales[:, b, cols],

@@ -14,6 +14,7 @@ U8 = mybir.dt.uint8
 FP8X4 = mybir.dt.float8_e4m3fn_x4
 FP4X4 = mybir.dt.float4_e2m1fn_x4
 MULT = mybir.AluOpType.mult
+ADD = mybir.AluOpType.add
 TANH = mybir.ActivationFunctionType.Tanh
 
 P = 128
@@ -32,57 +33,49 @@ def tile_list_gmlpt_tanh_gate_kernel(
         def sb(shape, dtype, name, tag=None):
             return keep.tile(shape, dtype, name=name, tag=tag or name, align_bytes=64)
 
+        def at(offset, shape, dtype, name):
+            return placed.tile(shape, dtype, name=name, offset=offset, align_bytes=64)
+
+        def bank(index, shape):
+            return psum.tile(shape, F32, name=f"bank{index}", tag=f"bank{index}", bufs=1)
+
         offsets = keep.tile([P, J // 16], U16, name="offsets")
         tab_s = sb([P, 2, T // 4], I32, "tab_s")
-        wg_early = sb([P, 2, HALF // 2], I32, "wg_early")
+        tab_w = sb([P, T], I32, "tab_w")
+        w_s = [sb([P, 2, R // 4], I32, f"w_s{m}") for m in range(2)]
+        w_early = [sb([P, 2, HALF // 2], I32, f"w_early{m}") for m in range(2)]
+        w_late = [sb([P, 2, HALF // 2], I32, f"w_late{m}") for m in range(2)]
+        gate = [sb([P, T], F32, f"gate{c}") for c in range(2)]
+        wd_raw = [sb([P, 4, N], F32, f"wd_raw{b}") for b in range(2)]
         ident = sb([P, P], F32, "ident")
         zero_in = sb([P, P], F32, "zero_in")
         zero = sb([P, P], F32, "zero")
-
-        def at(offset, shape, dtype, name):
-            return placed.tile(shape, dtype, name=name, offset=offset, align_bytes=64)
+        warm_in = sb([P, 4 * P], BF16, "warm_in")
+        warm_codes = sb([P, P], U32, "warm_codes")
+        warm_scales = sb([P, P], U8, "warm_scales")
 
         def load_scales(dst, src):
             rows = src.bitcast(I32).rearrange("a (q r) c -> r q a c", r=4)
             for r in range(4):
                 nc.sync.dma_start(out=dst[r:P:32], in_=rows[r])
 
-        def load_words(dst, m, b):
+        def load_words(dst, m, b, passes=slice(0, 2)):
             src = (wg_words, wu_words)[m].bitcast(I32).rearrange("a p c -> p a c")
-            nc.sync.dma_start(out=dst, in_=src[:, :, b * (HALF // 2) : (b + 1) * (HALF // 2)])
+            nc.sync.dma_start(out=dst[:, passes], in_=src[:, passes, b * (HALF // 2) : (b + 1) * (HALF // 2)])
 
-        tab_w = sb([P, T], I32, "tab_w")
-        w_s = [sb([P, 2, R // 4], I32, f"w_s{m}") for m in range(2)]
-        wu_early = sb([P, 2, HALF // 2], I32, "wu_early")
-        w_late = [sb([P, 2, HALF // 2], I32, f"w_late{m}") for m in range(2)]
-        gate = sb([P, 2, T], F32, "gate")
-        wd_raw = [sb([P, 4, N], F32, f"wd_raw{b}") for b in range(2)]
-        nc.vector.memset(tab_s[:, 0], 0)
-        nc.gpsimd.memset(tab_s[:, 1], 0)
-        nc.vector.memset(zero_in[:], 0.0)
-        nc.scalar.activation(out=zero[:], in_=zero_in[:], func=TANH)
-        nc.vector.memset(w_s[0][:], 0)
-        nc.gpsimd.memset(w_s[1][:], 0)
-        nc.gpsimd.affine_select(
-            out=ident[:], in_=zero[:], pattern=[[-1, P]], compare_op=mybir.AluOpType.not_equal, fill=1.0, base=0, channel_multiplier=1
-        )
+        def load_table():
+            nc.sync.dma_start(out=tab_w[:], in_=tab_words[0].rearrange("p t d -> p (t d)").bitcast(I32))
 
-        nc.sync.dma_start(offsets[:], offs)
-        load_words(wg_early[:], 0, 0)
-        load_scales(tab_s, tab_scales)
-        nc.sync.dma_start(out=tab_w[:], in_=tab_words[0].rearrange("p t d -> p (t d)").bitcast(I32))
-        load_words(w_late[0][:], 0, 1)
-        load_scales(w_s[0], wg_scales)
-        load_words(wu_early[:], 1, 0)
-        nc.sync.dma_start(out=gate[:, 0, :], in_=gT[:P, :])
-        nc.sync.dma_start(out=gate[:, 1, :], in_=gT[P:, :])
-        load_scales(w_s[1], wu_scales)
-        load_words(w_late[1][:], 1, 1)
-        nc.sync.dma_start(out=wd_raw[0][:], in_=wd[:HALF].rearrange("(p t) n -> p t n", t=4))
-        late_rows = wd[HALF:].rearrange("(q t i) n -> t q i n", t=4, i=8)
-        for t in range(4):
-            nc.sync.dma_start(out=wd_raw[1][:, t, :], in_=late_rows[t])
-        w_early = [wg_early, wu_early]
+        def load_gate(c):
+            nc.sync.dma_start(out=gate[c][:], in_=gT[P * c : P * (c + 1), :])
+
+        def load_wd(b):
+            if b == 0:
+                nc.sync.dma_start(out=wd_raw[0][:], in_=wd[:HALF].rearrange("(p t) n -> p t n", t=4))
+            else:
+                late_rows = wd[HALF:].rearrange("(q t i) n -> t q i n", t=4, i=8)
+                for t in range(4):
+                    nc.sync.dma_start(out=wd_raw[1][:, t, :], in_=late_rows[t])
 
         tab_s8 = tab_s[:].bitcast(U8)
 
@@ -90,14 +83,15 @@ def tile_list_gmlpt_tanh_gate_kernel(
             return offsets[:, j0 // 16 : j1 // 16]
 
         stat_w, stat_s = {}, {}
-
-        def pick_scales(picked, j0, j1):
-            for a in range(2):
-                nc.vector.tensor_copy(out=picked[:, a, j0 % 256 : j0 % 256 + j1 - j0], in_=tab_s8[:, a, :].indirect(lst(j0, j1)))
-            for jt in range(j0 // P, j1 // P):
-                stat_s[jt] = picked[:, :, P * (jt % 2) : P * (jt % 2 + 1)]
-
         parted = [sb([P, 2, 4 * P], U8, f"parted{i}") for i in range(2)]
+        pair_s = {}
+
+        def pick_scales(i, picked):
+            pair_s[i] = picked
+            for a in range(2):
+                nc.vector.tensor_copy(out=picked[:, a, :], in_=tab_s8[:, a, :].indirect(lst(256 * i, 256 * (i + 1))))
+            for jt in (2 * i, 2 * i + 1):
+                stat_s[jt] = picked[:, :, P * (jt % 2) : P * (jt % 2 + 1)]
 
         def pick_words(jt, words):
             stat_w[jt] = parted[jt // 2][:, :, 2 * P * (jt % 2) : 2 * P * (jt % 2 + 1)]
@@ -108,27 +102,25 @@ def tile_list_gmlpt_tanh_gate_kernel(
         h_cols = [sb([P, J, 4], BF16, f"h_cols{b}") for b in range(2)]
         h_codes = sb([P, 2, J], U32, "h_codes")
         h_scales = sb([P, 2, J], U8, "h_scales")
-        dealt_w = [sb([P, 2, 4, P // 2], I32, f"dealt_w{m}") for m in range(2)]
+        dealt_w = [[sb([P, 2, 2, P // 2], I32, f"dealt_w{m}{u}") for u in range(2)] for m in range(2)]
         dealt_s = [sb([P, 2, 4, P // 4], I32, f"dealt_s{m}") for m in range(2)]
         th = {}
 
-        def bank(shape, own=None):
-            if own is not None:
-                return psum.tile(shape, F32, name="own_bank", tag=f"own_bank{own}", bufs=1)
-            return psum.tile(shape, F32, name="bank", tag="bank", bufs=6)
-
-        def deal(m):
+        def deal_scales(m):
             nc.gpsimd.tensor_copy(
                 out=dealt_s[m][:].rearrange("p a t (q e) -> p a t q e", e=2),
                 in_=w_s[m][:, :, HALF // 4 :].rearrange("p a (q t e) -> p a t q e", t=4, e=2),
             )
-            nc.gpsimd.tensor_copy(
-                out=dealt_w[m][:].rearrange("p a t (q e) -> p a t q e", e=4),
-                in_=w_late[m][:].rearrange("p a (q t e) -> p a t q e", t=4, e=4),
-            )
 
-        def early_product(m, jt):
-            acc = bank([P, HALF], jt if m == 1 and jt < 2 else None)
+        def deal_words(m):
+            for u in range(2):
+                nc.gpsimd.tensor_copy(
+                    out=dealt_w[m][u][:].rearrange("p a t (q e) -> p a t q e", e=4),
+                    in_=w_late[m][:].rearrange("p a (q t e) -> p a t q e", t=4, e=4)[:, :, 2 * u : 2 * u + 2],
+                )
+
+        def early_product(m, jt, index):
+            acc = bank(index, [P, HALF])
             for a in range(2):
                 nc.tensor.matmul_mx(
                     out=acc[:],
@@ -141,20 +133,26 @@ def tile_list_gmlpt_tanh_gate_kernel(
                 )
             return acc[:].rearrange("j (p u e) -> j u p e", u=2, e=2)
 
-        def early_gate(jt):
-            ga = early_product(0, jt)
+        def early_gate(jt, index):
+            ga = early_product(0, jt, index)
             th[jt, 0] = sb([P, 2, P, 2], F32, f"th{jt}0")
             nc.scalar.activation(out=th[jt, 0][:], in_=ga, func=TANH)
 
-        def early_up(jt):
-            ub = early_product(1, jt)
-            nc.vector.tensor_tensor(out=h_rows[jt][:].rearrange("j (u p e) -> j u p e", u=2, e=2), in0=ub, in1=th[jt, 0][:], op=MULT)
+        def early_up(jt, index, aside=False):
+            ub = early_product(1, jt, index)
+            rows = h_rows[jt][:].rearrange("j (u p e) -> j u p e", u=2, e=2)
+            if aside:
+                ub_sb = sb([P, 2, P, 2], F32, f"ub_sb{jt}")
+                nc.scalar.copy(out=ub_sb[:], in_=ub)
+                nc.gpsimd.tensor_tensor(out=rows, in0=ub_sb[:], in1=th[jt, 0][:], op=MULT)
+            else:
+                nc.vector.tensor_tensor(out=rows, in0=ub, in1=th[jt, 0][:], op=MULT)
 
         def late_pass(out_ap, m, t, words, scales):
             for a in range(2):
                 nc.tensor.matmul_mx(
                     out=out_ap,
-                    lhsT=dealt_w[m][:, a, t, :].bitcast(U8).bitcast(FP4X4),
+                    lhsT=dealt_w[m][t // 2][:, a, t % 2, :].bitcast(U8).bitcast(FP4X4),
                     lhsT_scale=dealt_s[m][:, a, t, :].bitcast(U8),
                     rhs=words[:, a, :].bitcast(FP4X4),
                     rhs_scale=scales[:, a, :],
@@ -162,18 +160,19 @@ def tile_list_gmlpt_tanh_gate_kernel(
                     stop=(a == 1),
                 )
 
-        def late_gate(i):
+        def late_gate(i, indices, last_by_tile=False):
             th[i, 1] = sb([P, 4, 2 * P], F32, f"th{i}1")
             for u in range(2):
-                ga = bank([P, 2, 2 * P], u if i == 1 else None)
+                ga = bank(indices[u], [P, 2, 2 * P])
                 for e in range(2):
                     late_pass(ga[:, e, :], 0, 2 * u + e, parted[i][:], pair_s[i][:])
-                nc.scalar.activation(out=th[i, 1][:, 2 * u : 2 * u + 2, :], in_=ga[:], func=TANH)
+                for j0, j1 in ((0, P), (P, 2 * P)) if last_by_tile and u == 1 else ((0, 2 * P),):
+                    nc.scalar.activation(out=th[i, 1][:, 2 * u : 2 * u + 2, j0:j1], in_=ga[:, :, j0:j1], func=TANH)
 
         ub_late = {}
 
-        def late_up(jt):
-            ub_late[jt] = bank([P, 4, P])
+        def late_up(jt, index):
+            ub_late[jt] = bank(index, [P, 4, P])
             for t in range(4):
                 late_pass(ub_late[jt][:, t, :], 1, t, stat_w[jt], stat_s[jt])
 
@@ -185,14 +184,14 @@ def tile_list_gmlpt_tanh_gate_kernel(
                 op=MULT,
             )
 
-        def turn(jt0, jt1):
-            turned = bank([P, 2, 2, P])
-            for jt in range(jt0, jt1):
+        def turn(jt0, index):
+            turned = bank(index, [P, 2, 2, P])
+            for jt in range(jt0, jt0 + 2):
                 words = h_rows[jt][:].bitcast(F32)
                 for u in range(2):
                     nc.tensor.transpose(turned[:, jt - jt0, u, :], words[:, P * u : P * (u + 1)], ident[:])
             nc.scalar.copy(
-                out=h_cols[0][:].bitcast(F32)[:, P * jt0 : P * jt1, :].rearrange("p (i c k) u -> p i c u k", i=2, k=2),
+                out=h_cols[0][:].bitcast(F32)[:, P * jt0 : P * (jt0 + 2), :].rearrange("p (i c k) u -> p i c u k", i=2, k=2),
                 in_=turned[:].rearrange("p i u (c k) -> p i c u k", k=2),
             )
 
@@ -203,120 +202,145 @@ def tile_list_gmlpt_tanh_gate_kernel(
                 in_=h_cols[b][:, j0:j1, :].rearrange("p j t -> p (j t)"),
             )
 
+        wd_bf = [sb([P, N, 4], BF16, f"wd_bf{b}") for b in range(2)]
 
-        def prepare_wd(b, c, tag):
+        def round_wd(b, c, copy):
             cols = slice(P * c, P * (c + 1))
-            wd_bf = sb([P, P, 4], BF16, f"wd_bf{b}{c}", tag)
-            if b == 0:
-                nc.scalar.copy(out=wd_bf[:].rearrange("p (c i) t -> p c t i", i=2), in_=wd_raw[b][:, :, cols].rearrange("p t (c i) -> p c t i", i=2))
-            else:
-                nc.gpsimd.tensor_scalar(out=wd_bf[:], in0=wd_raw[b][:, :, cols].rearrange("p t n -> p n t"), scalar1=1.0, scalar2=0.0, op0=MULT, op1=mybir.AluOpType.add)
-            nc.vector.quantize_mx(
-                out=wd_codes[:, b, cols].bitcast(FP8X4),
-                scales=wd_scales[:, b, cols],
-                in_=wd_bf[:].rearrange("p n t -> p (n t)"),
+            copy(out=wd_bf[b][:, cols, :].rearrange("p (c i) t -> p c t i", i=2), in_=wd_raw[b][:, :, cols].rearrange("p t (c i) -> p c t i", i=2))
+
+        def round_wd_aside(b, c):
+            cols = slice(P * c, P * (c + 1))
+            nc.gpsimd.tensor_scalar(
+                out=wd_bf[b][:, cols, :], in0=wd_raw[b][:, :, cols].rearrange("p t n -> p n t"), scalar1=1.0, scalar2=0.0, op0=MULT, op1=ADD
             )
+
+        def quantise_wd(b):
+            nc.vector.quantize_mx(out=wd_codes[b][:].bitcast(FP8X4), scales=wd_scales[b][:], in_=wd_bf[b][:].rearrange("p n t -> p (n t)"))
 
         picked_g = sb([P, 2, J], F32, "picked_g")
 
         def pick_gate(c, j0, j1):
-            nc.vector.tensor_copy(out=picked_g[:, c, j0:j1], in_=gate[:, c, :].indirect(lst(j0, j1)))
+            nc.vector.tensor_copy(out=picked_g[:, c, j0:j1], in_=gate[c][:].indirect(lst(j0, j1)))
 
         out_view = out.rearrange("(c p) j -> p c j", c=2)
 
         def down_pass(y, c, b, j0, j1):
             nc.tensor.matmul_mx(
                 out=y,
-                lhsT=wd_codes[:, b, P * c : P * (c + 1)].bitcast(FP8X4),
-                lhsT_scale=wd_scales[:, b, P * c : P * (c + 1)],
+                lhsT=wd_codes[b][:, P * c : P * (c + 1)].bitcast(FP8X4),
+                lhsT_scale=wd_scales[b][:, P * c : P * (c + 1)],
                 rhs=h_codes[:, b, j0:j1].bitcast(FP8X4),
                 rhs_scale=h_scales[:, b, j0:j1],
                 start=(b == 0),
                 stop=(b == 1),
             )
 
-        def second_layer(j0, j1, tag):
-            y = bank([P, 2, j1 - j0])
+        def down(j0, j1, index):
+            y = bank(index, [P, 2, j1 - j0])
             for c in range(2):
                 for b in range(2):
                     down_pass(y[:, c, :], c, b, j0, j1)
-            res = sb([P, 2, j1 - j0], F32, f"res{j0}", tag)
-            nc.vector.tensor_tensor(out=res[:], in0=y[:], in1=picked_g[:, :, j0:j1], op=MULT)
-            nc.sync.dma_start(out=out_view[:, :, j0:j1], in_=res[:])
+            return y
 
-        def warm_up(passes):
-            acc = bank([P, HALF])
+        def finish(y, c0, c1, j0, j1, aside=False, queue=nc.sync, tag=None):
+            res = sb([P, c1 - c0, j1 - j0], F32, f"res{c0}_{j0}", tag)
+            if aside:
+                y_sb = sb([P, c1 - c0, j1 - j0], F32, f"y_sb{c0}_{j0}")
+                nc.scalar.copy(out=y_sb[:], in_=y)
+                nc.gpsimd.tensor_tensor(out=res[:], in0=y_sb[:], in1=picked_g[:, c0:c1, j0:j1], op=MULT)
+            else:
+                nc.vector.tensor_tensor(out=res[:], in0=y, in1=picked_g[:, c0:c1, j0:j1], op=MULT)
+            queue.dma_start(out=out_view[:, c0:c1, j0:j1], in_=res[:])
+
+        def warm_up(passes, index):
+            acc = bank(index, [P, P])
             for i in range(passes):
                 nc.tensor.matmul_mx(
                     out=acc[:],
-                    lhsT=wg_early[:, 0, : P // 2].bitcast(U8).bitcast(FP4X4),
-                    lhsT_scale=tab_s8[:, 0, :P],
-                    rhs=wg_early[:, 0, :].bitcast(U8).bitcast(FP4X4),
-                    rhs_scale=tab_s8[:, 0, :HALF],
+                    lhsT=warm_codes[:].bitcast(FP8X4),
+                    lhsT_scale=warm_scales[:],
+                    rhs=warm_codes[:].bitcast(FP8X4),
+                    rhs_scale=warm_scales[:],
                     start=(i == 0),
                     stop=(i == passes - 1),
                 )
 
-        pair_s = [sb([P, 2, 256], U8, "picked_s0")]
-        pick_scales(pair_s[0], 0, 256)
-        warm_up(3)
+        nc.gpsimd.memset(tab_s[:], 0)
+        nc.vector.memset(zero_in[:], 0.0)
+        nc.scalar.activation(out=zero[:], in_=zero_in[:], func=TANH)
+        nc.vector.memset(w_s[0][:], 0)
+        nc.vector.memset(w_s[1][:], 0)
+        nc.vector.memset(warm_in[:].bitcast(I32), 0)
+        nc.vector.quantize_mx(out=warm_codes[:].bitcast(FP8X4), scales=warm_scales[:], in_=warm_in[:])
+        nc.gpsimd.affine_select(
+            out=ident[:], in_=zero[:], pattern=[[-1, P]], compare_op=mybir.AluOpType.not_equal, fill=1.0, base=0, channel_multiplier=1
+        )
+        nc.sync.dma_start(offsets[:], offs)
+        load_words(w_early[0], 0, 0, slice(0, 1))
+        load_scales(tab_s, tab_scales)
+        load_table()
+        load_words(w_early[0], 0, 0, slice(1, 2))
+        load_scales(w_s[0], wg_scales)
+        load_words(w_late[0], 0, 1)
+        load_gate(0)
+        load_words(w_early[1], 1, 0)
+        load_gate(1)
+        load_scales(w_s[1], wu_scales)
+        load_words(w_late[1], 1, 1)
+        load_wd(0)
+        load_wd(1)
+
+        warm_up(14, 7)
+        pick_scales(0, sb([P, 2, 256], U8, "picked_s0"))
         pick_words(0, at(256, [P, P], U32, "picked_w0"))
         pick_words(1, sb([P, P], U32, "picked_w1"))
-        early_gate(0)
-        early_gate(1)
-        deal(0)
-        late_gate(0)
+        early_gate(0, 0)
+        early_gate(1, 1)
+        deal_scales(0)
+        deal_words(0)
+        late_gate(0, (2, 3))
         pick_words(2, at(640, [P, P], U32, "picked_w2"))
-        pair_s.append(at(0, [P, 2, 256], U8, "picked_s1"))
-        pick_scales(pair_s[1], 256, 512)
-        early_gate(2)
+        pick_scales(1, at(0, [P, 2, 256], U8, "picked_s1"))
+        early_gate(2, 0)
         pick_words(3, sb([P, P], U32, "picked_w3", "picked_w1"))
-        early_gate(3)
+        early_gate(3, 1)
         pick_gate(0, 0, 512)
         pick_gate(1, 0, 512)
         for jt in range(4):
-            early_up(jt)
-        deal(1)
-        wd_codes = sb([P, 2, N], U32, "wd_codes", "th10")
-        wd_scales = sb([P, 2, N], U8, "wd_scales")
-        prepare_wd(0, 0, None)
-        prepare_wd(0, 1, None)
-        late_up(0)
-        late_up(1)
-        turn(0, 2)
-        turn(2, 4)
+            early_up(jt, 4 + jt)
+        deal_scales(1)
+        deal_words(1)
+        wd_codes = [sb([P, N], U32, "wd_codes0", "th10"), sb([P, N], U32, "wd_codes1")]
+        wd_scales = [sb([P, N], U8, f"wd_scales{b}") for b in range(2)]
+        for c in range(2):
+            round_wd(0, c, nc.scalar.copy)
+        late_up(0, 2)
+        late_up(1, 3)
+        turn(0, 0)
+        turn(2, 1)
         late_mult(0)
-        prepare_wd(1, 0, None)
-        prepare_wd(1, 1, None)
+        quantise_wd(0)
+        for c in range(2):
+            round_wd_aside(1, c)
         late_mult(1)
+        quantise_wd(1)
         quantise_h(0, 0, 256)
-        late_gate(1)
-        late_up(2)
-        late_up(3)
-        quantise_h(0, 256, 512)
+        late_gate(1, (4, 5), last_by_tile=True)
+        late_up(2, 6)
+        late_up(3, 7)
         quantise_h(1, 0, 256)
+        quantise_h(0, 256, 512)
         late_mult(2)
         late_mult(3)
         quantise_h(1, 256, 384)
         quantise_h(1, 384, 512)
-        y = bank([P, 2, 256])
+        y = down(0, 256, 2)
+        finish(y[:, 0:1, :], 0, 1, 0, 256)
+        finish(y[:, 1:2, :], 1, 2, 0, 256)
+        last_y = [bank(c, [P, 1, P]) for c in range(2)]
         for c in range(2):
-            for b in range(2):
-                down_pass(y[:, c, :], c, b, 0, 256)
-        y_sb = sb([P, 256], F32, "y_sb")
-        nc.scalar.copy(out=y_sb[:], in_=y[:, 1, :])
-        res_g = sb([P, 256], F32, "res_g")
-        nc.gpsimd.tensor_tensor(out=res_g[:], in0=y_sb[:], in1=picked_g[:, 1, :256], op=MULT)
-        nc.scalar.dma_start(out=out_view[:, 1, :256], in_=res_g[:])
-        res_v = sb([P, 256], F32, "res_v")
-        nc.vector.tensor_tensor(out=res_v[:], in0=y[:, 0, :], in1=picked_g[:, 0, :256], op=MULT)
-        nc.sync.dma_start(out=out_view[:, 0, :256], in_=res_v[:])
-        last_y = [bank([P, P]) for c in range(2)]
+            down_pass(last_y[c][:, 0, :], c, 0, 384, 512)
+        finish(down(256, 384, 3)[:], 0, 2, 256, 384)
         for c in range(2):
-            down_pass(last_y[c][:], c, 0, 384, 512)
-        second_layer(256, 384, None)
-        res = sb([P, 2, P], F32, "res_last")
-        for c in range(2):
-            down_pass(last_y[c][:], c, 1, 384, 512)
-            nc.vector.tensor_tensor(out=res[:, c, :], in0=last_y[c][:], in1=picked_g[:, c, 384:512], op=MULT)
-            nc.sync.dma_start(out=out_view[:, c, 384:512], in_=res[:, c, :])
+            down_pass(last_y[c][:, 0, :], c, 1, 384, 512)
+            finish(last_y[c][:], c, c + 1, 384, 512)

@@ -43,16 +43,15 @@ def tile_list_gmlpt_tanh_gate_kernel(
         tab_s = sb([P, 2, T // 4], I32, "tab_s")
         tab_w = sb([P, T], I32, "tab_w")
         w_s = [sb([P, 2, R // 4], I32, f"w_s{m}") for m in range(2)]
-        w_early = [sb([P, 2, HALF // 2], I32, f"w_early{m}") for m in range(2)]
+        wg_early = [sb([P, 1, HALF // 2], I32, f"wg_early{a}") for a in range(2)]
+        wu_early = sb([P, 2, HALF // 2], I32, "wu_early")
+        w_early = [[wg_early[a][:, 0, :] for a in range(2)], [wu_early[:, a, :] for a in range(2)]]
         w_late = [sb([P, 2, HALF // 2], I32, f"w_late{m}") for m in range(2)]
-        gate = [sb([P, T], F32, f"gate{c}") for c in range(2)]
+        gate = [sb([P, T], F32, "gate0"), at(2048, [P, T], F32, "gate1")]
         wd_raw = [sb([P, 4, N], F32, f"wd_raw{b}") for b in range(2)]
         ident = sb([P, P], F32, "ident")
         zero_in = sb([P, P], F32, "zero_in")
         zero = sb([P, P], F32, "zero")
-        warm_in = sb([P, 4 * P], BF16, "warm_in")
-        warm_codes = sb([P, P], U32, "warm_codes")
-        warm_scales = sb([P, P], U8, "warm_scales")
 
         def load_scales(dst, src):
             rows = src.bitcast(I32).rearrange("a (q r) c -> r q a c", r=4)
@@ -61,7 +60,7 @@ def tile_list_gmlpt_tanh_gate_kernel(
 
         def load_words(dst, m, b, passes=slice(0, 2)):
             src = (wg_words, wu_words)[m].bitcast(I32).rearrange("a p c -> p a c")
-            nc.sync.dma_start(out=dst[:, passes], in_=src[:, passes, b * (HALF // 2) : (b + 1) * (HALF // 2)])
+            nc.sync.dma_start(out=dst[:], in_=src[:, passes, b * (HALF // 2) : (b + 1) * (HALF // 2)])
 
         def load_table():
             nc.sync.dma_start(out=tab_w[:], in_=tab_words[0].rearrange("p t d -> p (t d)").bitcast(I32))
@@ -99,7 +98,7 @@ def tile_list_gmlpt_tanh_gate_kernel(
             nc.vector.tensor_copy(out=stat_w[jt].bitcast(U16), in_=words[:].bitcast(U16).rearrange("p (j d) -> p d j", d=2))
 
         h_rows = [sb([P, HALF], BF16, f"h_rows{jt}") for jt in range(4)]
-        h_cols = [sb([P, J, 4], BF16, f"h_cols{b}") for b in range(2)]
+        h_cols = [[sb([P, 2 * P, 4], BF16, f"h_cols{b}{i}") for i in range(2)] for b in range(2)]
         h_codes = sb([P, 2, J], U32, "h_codes")
         h_scales = sb([P, 2, J], U8, "h_scales")
         dealt_w = [[sb([P, 2, 2, P // 2], I32, f"dealt_w{m}{u}") for u in range(2)] for m in range(2)]
@@ -126,7 +125,7 @@ def tile_list_gmlpt_tanh_gate_kernel(
                     out=acc[:],
                     lhsT=stat_w[jt][:, a, :].bitcast(FP4X4),
                     lhsT_scale=stat_s[jt][:, a, :],
-                    rhs=w_early[m][:, a, :].bitcast(U8).bitcast(FP4X4),
+                    rhs=w_early[m][a].bitcast(U8).bitcast(FP4X4),
                     rhs_scale=w_s[m][:].bitcast(U8)[:, a, :HALF],
                     start=(a == 0),
                     stop=(a == 1),
@@ -178,7 +177,7 @@ def tile_list_gmlpt_tanh_gate_kernel(
 
         def late_mult(jt):
             nc.vector.tensor_tensor(
-                out=h_cols[1][:, P * jt : P * (jt + 1), :].rearrange("p (c i) t -> p c t i", i=2),
+                out=h_cols[1][jt // 2][:, P * (jt % 2) : P * (jt % 2 + 1), :].rearrange("p (c i) t -> p c t i", i=2),
                 in0=ub_late[jt][:].rearrange("p t (c i) -> p c t i", i=2),
                 in1=th[jt // 2, 1][:, :, P * (jt % 2) : P * (jt % 2 + 1)].rearrange("p t (c i) -> p c t i", i=2),
                 op=MULT,
@@ -191,7 +190,7 @@ def tile_list_gmlpt_tanh_gate_kernel(
                 for u in range(2):
                     nc.tensor.transpose(turned[:, jt - jt0, u, :], words[:, P * u : P * (u + 1)], ident[:])
             nc.scalar.copy(
-                out=h_cols[0][:].bitcast(F32)[:, P * jt0 : P * (jt0 + 2), :].rearrange("p (i c k) u -> p i c u k", i=2, k=2),
+                out=h_cols[0][jt0 // 2][:].bitcast(F32).rearrange("p (i c k) u -> p i c u k", i=2, k=2),
                 in_=turned[:].rearrange("p i u (c k) -> p i c u k", k=2),
             )
 
@@ -199,7 +198,7 @@ def tile_list_gmlpt_tanh_gate_kernel(
             nc.vector.quantize_mx(
                 out=h_codes[:, b, j0:j1].bitcast(FP8X4),
                 scales=h_scales[:, b, j0:j1],
-                in_=h_cols[b][:, j0:j1, :].rearrange("p j t -> p (j t)"),
+                in_=h_cols[b][j0 // 256][:, j0 % 256 : j0 % 256 + j1 - j0, :].rearrange("p j t -> p (j t)"),
             )
 
         wd_bf = [sb([P, N, 4], BF16, f"wd_bf{b}") for b in range(2)]
@@ -257,10 +256,10 @@ def tile_list_gmlpt_tanh_gate_kernel(
             for i in range(passes):
                 nc.tensor.matmul_mx(
                     out=acc[:],
-                    lhsT=warm_codes[:].bitcast(FP8X4),
-                    lhsT_scale=warm_scales[:],
-                    rhs=warm_codes[:].bitcast(FP8X4),
-                    rhs_scale=warm_scales[:],
+                    lhsT=w_early[0][0][:, : P // 2].bitcast(U8).bitcast(FP4X4),
+                    lhsT_scale=tab_s8[:, 0, :P],
+                    rhs=w_early[0][0][:, : P // 2].bitcast(U8).bitcast(FP4X4),
+                    rhs_scale=tab_s8[:, 0, :P],
                     start=(i == 0),
                     stop=(i == passes - 1),
                 )
@@ -270,20 +269,18 @@ def tile_list_gmlpt_tanh_gate_kernel(
         nc.scalar.activation(out=zero[:], in_=zero_in[:], func=TANH)
         nc.vector.memset(w_s[0][:], 0)
         nc.vector.memset(w_s[1][:], 0)
-        nc.vector.memset(warm_in[:].bitcast(I32), 0)
-        nc.vector.quantize_mx(out=warm_codes[:].bitcast(FP8X4), scales=warm_scales[:], in_=warm_in[:])
         nc.gpsimd.affine_select(
             out=ident[:], in_=zero[:], pattern=[[-1, P]], compare_op=mybir.AluOpType.not_equal, fill=1.0, base=0, channel_multiplier=1
         )
         nc.sync.dma_start(offsets[:], offs)
-        load_words(w_early[0], 0, 0, slice(0, 1))
+        load_words(wg_early[0], 0, 0, slice(0, 1))
         load_scales(tab_s, tab_scales)
         load_table()
-        load_words(w_early[0], 0, 0, slice(1, 2))
+        load_words(wg_early[1], 0, 0, slice(1, 2))
         load_scales(w_s[0], wg_scales)
         load_words(w_late[0], 0, 1)
         load_gate(0)
-        load_words(w_early[1], 1, 0)
+        load_words(wu_early, 1, 0)
         load_gate(1)
         load_scales(w_s[1], wu_scales)
         load_words(w_late[1], 1, 1)
@@ -307,7 +304,7 @@ def tile_list_gmlpt_tanh_gate_kernel(
         pick_gate(0, 0, 512)
         pick_gate(1, 0, 512)
         for jt in range(4):
-            early_up(jt, 4 + jt)
+            early_up(jt, 4 + jt, aside=(jt == 0))
         deal_scales(1)
         deal_words(1)
         wd_codes = [sb([P, N], U32, "wd_codes0", "th10"), sb([P, N], U32, "wd_codes1")]
@@ -325,8 +322,8 @@ def tile_list_gmlpt_tanh_gate_kernel(
         late_mult(1)
         quantise_wd(1)
         quantise_h(0, 0, 256)
-        late_gate(1, (4, 5), last_by_tile=True)
-        late_up(2, 6)
+        late_gate(1, (5, 6), last_by_tile=True)
+        late_up(2, 4)
         late_up(3, 7)
         quantise_h(1, 0, 256)
         quantise_h(0, 256, 512)

@@ -47,7 +47,7 @@ def tile_list_gmlpt_tanh_gate_kernel(
         wu_early = sb([P, 2, HALF // 2], I32, "wu_early")
         w_early = [[wg_early[a][:, 0, :] for a in range(2)], [wu_early[:, a, :] for a in range(2)]]
         w_late = [sb([P, 2, HALF // 2], I32, f"w_late{m}") for m in range(2)]
-        gate = [sb([P, T], F32, "gate0"), at(2048, [P, T], F32, "gate1")]
+        gate = [sb([P, T], F32, f"gate{c}") for c in range(2)]
         wd_raw = [sb([P, 4, N], F32, f"wd_raw{b}") for b in range(2)]
         ident = sb([P, P], F32, "ident")
         zero_in = sb([P, P], F32, "zero_in")
@@ -102,7 +102,7 @@ def tile_list_gmlpt_tanh_gate_kernel(
         h_codes = sb([P, 2, J], U32, "h_codes")
         h_scales = sb([P, 2, J], U8, "h_scales")
         dealt_w = [[sb([P, 2, 2, P // 2], I32, f"dealt_w{m}{u}") for u in range(2)] for m in range(2)]
-        dealt_s = [sb([P, 2, 4, P // 4], I32, f"dealt_s{m}") for m in range(2)]
+        dealt_s = [sb([P, 2, 4, P // 4], I32, "dealt_s0", "gate0"), sb([P, 2, 4, P // 4], I32, "dealt_s1")]
         th = {}
 
         def deal_scales(m):
@@ -278,12 +278,12 @@ def tile_list_gmlpt_tanh_gate_kernel(
         load_table()
         load_words(wg_early[1], 0, 0, slice(1, 2))
         load_scales(w_s[0], wg_scales)
-        load_words(w_late[0], 0, 1)
         load_gate(0)
         load_words(wu_early, 1, 0)
-        load_gate(1)
         load_scales(w_s[1], wu_scales)
+        load_words(w_late[0], 0, 1)
         load_words(w_late[1], 1, 1)
+        load_gate(1)
         load_wd(0)
         load_wd(1)
 
@@ -293,39 +293,40 @@ def tile_list_gmlpt_tanh_gate_kernel(
         pick_words(1, sb([P, P], U32, "picked_w1"))
         early_gate(0, 0)
         early_gate(1, 1)
-        deal_scales(0)
-        deal_words(0)
-        late_gate(0, (2, 3))
         pick_words(2, at(640, [P, P], U32, "picked_w2"))
         pick_scales(1, at(0, [P, 2, 256], U8, "picked_s1"))
-        early_gate(2, 0)
+        early_gate(2, 2)
         pick_words(3, sb([P, P], U32, "picked_w3", "picked_w1"))
-        early_gate(3, 1)
+        early_gate(3, 3)
         pick_gate(0, 0, 512)
-        pick_gate(1, 0, 512)
-        for jt in range(4):
-            early_up(jt, 4 + jt, aside=(jt == 0))
-        deal_scales(1)
-        deal_words(1)
-        wd_codes = [sb([P, N], U32, "wd_codes0", "th10"), sb([P, N], U32, "wd_codes1")]
+        early_up(0, 4)
+        early_up(1, 5)
+        early_up(2, 6)
+        early_up(3, 7)
+        for m in range(2):
+            deal_scales(m)
+            deal_words(m)
+        wd_codes = [sb([P, N], U32, f"wd_codes{b}") for b in range(2)]
         wd_scales = [sb([P, N], U8, f"wd_scales{b}") for b in range(2)]
-        for c in range(2):
-            round_wd(0, c, nc.scalar.copy)
+        late_gate(0, (0, 1))
         late_up(0, 2)
         late_up(1, 3)
+        for c in range(2):
+            round_wd(0, c, nc.scalar.copy)
+        quantise_wd(0)
+        pick_gate(1, 0, 512)
+        round_wd_aside(1, 0)
+        round_wd(1, 1, nc.vector.tensor_copy)
         turn(0, 0)
         turn(2, 1)
         late_mult(0)
-        quantise_wd(0)
-        for c in range(2):
-            round_wd_aside(1, c)
         late_mult(1)
         quantise_wd(1)
-        quantise_h(0, 0, 256)
-        late_gate(1, (5, 6), last_by_tile=True)
-        late_up(2, 4)
-        late_up(3, 7)
         quantise_h(1, 0, 256)
+        quantise_h(0, 0, 256)
+        late_gate(1, (4, 5), last_by_tile=True)
+        late_up(2, 6)
+        late_up(3, 7)
         quantise_h(0, 256, 512)
         late_mult(2)
         late_mult(3)

@@ -92,10 +92,13 @@ def tile_list_gmlpt_tanh_gate_kernel(
             for jt in (2 * i, 2 * i + 1):
                 stat_s[jt] = picked[:, :, P * (jt % 2) : P * (jt % 2 + 1)]
 
-        def pick_words(jt, words):
-            stat_w[jt] = parted[jt // 2][:, :, 2 * P * (jt % 2) : 2 * P * (jt % 2 + 1)]
-            nc.vector.tensor_copy(out=words[:], in_=tab_w[:].bitcast(U32).indirect(lst(P * jt, P * (jt + 1))))
-            nc.vector.tensor_copy(out=stat_w[jt].bitcast(U16), in_=words[:].bitcast(U16).rearrange("p (j d) -> p d j", d=2))
+        def pick_words(i, words):
+            for jt in (2 * i, 2 * i + 1):
+                stat_w[jt] = parted[i][:, :, 2 * P * (jt % 2) : 2 * P * (jt % 2 + 1)]
+            nc.vector.tensor_copy(out=words[:], in_=tab_w[:].bitcast(U32).indirect(lst(256 * i, 256 * (i + 1))))
+
+        def part_words(i, words):
+            nc.vector.tensor_copy(out=parted[i][:].bitcast(U16), in_=words[:].bitcast(U16).rearrange("p (j d) -> p d j", d=2))
 
         h_rows = [sb([P, HALF], BF16, f"h_rows{jt}") for jt in range(4)]
         h_cols = [[sb([P, 2 * P, 4], BF16, f"h_cols{b}{i}") for i in range(2)] for b in range(2)]
@@ -288,16 +291,15 @@ def tile_list_gmlpt_tanh_gate_kernel(
         load_wd(1)
 
         warm_up(14, 7)
+        picked_w = [sb([P, 256], U32, f"picked_w{i}") for i in range(2)]
         pick_scales(0, sb([P, 2, 256], U8, "picked_s0"))
-        pick_words(0, at(256, [P, P], U32, "picked_w0"))
-        pick_words(1, sb([P, P], U32, "picked_w1"))
-        early_gate(0, 0)
-        early_gate(1, 1)
-        pick_words(2, at(640, [P, P], U32, "picked_w2"))
-        pick_scales(1, at(0, [P, 2, 256], U8, "picked_s1"))
-        early_gate(2, 2)
-        pick_words(3, sb([P, P], U32, "picked_w3", "picked_w1"))
-        early_gate(3, 3)
+        pick_words(0, picked_w[0])
+        pick_words(1, picked_w[1])
+        part_words(0, picked_w[0])
+        part_words(1, picked_w[1])
+        pick_scales(1, sb([P, 2, 256], U8, "picked_s1", "picked_w0"))
+        for jt in range(4):
+            early_gate(jt, jt)
         pick_gate(0, 0, 512)
         early_up(0, 4)
         early_up(1, 5)

@@ -100,40 +100,60 @@ def tile_list_gmlpt_tanh_gate_kernel(
         def part_words(i, words):
             nc.vector.tensor_copy(out=parted[i][:].bitcast(U16), in_=words[:].bitcast(U16).rearrange("p (j d) -> p d j", d=2))
 
+        def pick_tile_words(jt, words):
+            stat_w[jt] = parted[jt // 2][:, :, 2 * P * (jt % 2) : 2 * P * (jt % 2 + 1)]
+            nc.vector.tensor_copy(out=words[:], in_=tab_w[:].bitcast(U32).indirect(lst(P * jt, P * (jt + 1))))
+
+        def part_tile_words(jt, words):
+            nc.vector.tensor_copy(out=stat_w[jt].bitcast(U16), in_=words[:].bitcast(U16).rearrange("p (j d) -> p d j", d=2))
+
         h_rows = [sb([P, HALF], BF16, f"h_rows{jt}") for jt in range(4)]
         h_cols = [[sb([P, 2 * P, 4], BF16, f"h_cols{b}{i}") for i in range(2)] for b in range(2)]
         h_codes = sb([P, 2, J], U32, "h_codes")
         h_scales = sb([P, 2, J], U8, "h_scales")
-        dealt_w = [[sb([P, 2, 2, P // 2], I32, f"dealt_w{m}{u}") for u in range(2)] for m in range(2)]
-        dealt_s = [sb([P, 2, 4, P // 4], I32, "dealt_s0", "gate0"), sb([P, 2, 4, P // 4], I32, "dealt_s1")]
+        dealt_w = [[sb([P, 2, 2, P // 2], I32, f"dealt_w{m}{u}", "gate0" if (m, u) == (1, 0) else None) for u in range(2)] for m in range(2)]
+        dealt_s = []
         th = {}
 
         def deal_scales(m):
-            nc.gpsimd.tensor_copy(
+            nc.vector.tensor_copy(
                 out=dealt_s[m][:].rearrange("p a t (q e) -> p a t q e", e=2),
                 in_=w_s[m][:, :, HALF // 4 :].rearrange("p a (q t e) -> p a t q e", t=4, e=2),
             )
 
         def deal_words(m):
             for u in range(2):
-                nc.gpsimd.tensor_copy(
+                (nc.vector, nc.gpsimd)[m].tensor_copy(
                     out=dealt_w[m][u][:].rearrange("p a t (q e) -> p a t q e", e=4),
                     in_=w_late[m][:].rearrange("p a (q t e) -> p a t q e", t=4, e=4)[:, :, 2 * u : 2 * u + 2],
                 )
 
-        def early_product(m, jt, index):
-            acc = bank(index, [P, HALF])
+        def early_passes(acc, m, jt, r0, r1):
             for a in range(2):
                 nc.tensor.matmul_mx(
-                    out=acc[:],
+                    out=acc,
                     lhsT=stat_w[jt][:, a, :].bitcast(FP4X4),
                     lhsT_scale=stat_s[jt][:, a, :],
-                    rhs=w_early[m][a].bitcast(U8).bitcast(FP4X4),
-                    rhs_scale=w_s[m][:].bitcast(U8)[:, a, :HALF],
+                    rhs=w_early[m][a][:, r0 // 2 : r1 // 2].bitcast(U8).bitcast(FP4X4),
+                    rhs_scale=w_s[m][:].bitcast(U8)[:, a, r0:r1],
                     start=(a == 0),
                     stop=(a == 1),
                 )
-            return acc[:].rearrange("j (p u e) -> j u p e", u=2, e=2)
+            return acc.rearrange("j (p u e) -> j u p e", u=2, e=2)
+
+        def early_product(m, jt, index):
+            return early_passes(bank(index, [P, HALF])[:], m, jt, 0, HALF)
+
+        def shared_banks(up_jt, gate_jt, indices):
+            both = [bank(index, [P, 2, HALF // 2]) for index in indices]
+            ub = [early_passes(both[h][:, 0, :], 1, up_jt, 256 * h, 256 * (h + 1)) for h in range(2)]
+            ga = [early_passes(both[h][:, 1, :], 0, gate_jt, 256 * h, 256 * (h + 1)) for h in range(2)]
+            th[gate_jt, 0] = sb([P, 2, P, 2], F32, f"th{gate_jt}0")
+            rows = h_rows[up_jt][:].rearrange("j (u p e) -> j u p e", u=2, e=2)
+            for h in range(2):
+                part = slice(64 * h, 64 * (h + 1))
+                nc.scalar.activation(out=th[gate_jt, 0][:, :, part, :], in_=ga[h], func=TANH)
+                nc.vector.tensor_tensor(out=rows[:, :, part, :], in0=ub[h], in1=th[up_jt, 0][:, :, part, :], op=MULT)
 
         def early_gate(jt, index):
             ga = early_product(0, jt, index)
@@ -255,14 +275,14 @@ def tile_list_gmlpt_tanh_gate_kernel(
             queue.dma_start(out=out_view[:, c0:c1, j0:j1], in_=res[:])
 
         def warm_up(passes, index):
-            acc = bank(index, [P, P])
+            acc = bank(index, [P, 2 * P])
             for i in range(passes):
                 nc.tensor.matmul_mx(
                     out=acc[:],
                     lhsT=w_early[0][0][:, : P // 2].bitcast(U8).bitcast(FP4X4),
                     lhsT_scale=tab_s8[:, 0, :P],
-                    rhs=w_early[0][0][:, : P // 2].bitcast(U8).bitcast(FP4X4),
-                    rhs_scale=tab_s8[:, 0, :P],
+                    rhs=w_early[0][0][:, :P].bitcast(U8).bitcast(FP4X4),
+                    rhs_scale=tab_s8[:, 0, : 2 * P],
                     start=(i == 0),
                     stop=(i == passes - 1),
                 )
@@ -281,63 +301,69 @@ def tile_list_gmlpt_tanh_gate_kernel(
         load_table()
         load_words(wg_early[1], 0, 0, slice(1, 2))
         load_scales(w_s[0], wg_scales)
-        load_gate(0)
         load_words(wu_early, 1, 0)
         load_scales(w_s[1], wu_scales)
+        load_gate(0)
         load_words(w_late[0], 0, 1)
         load_words(w_late[1], 1, 1)
-        load_gate(1)
         load_wd(0)
+        load_gate(1)
         load_wd(1)
 
-        warm_up(14, 7)
-        picked_w = [sb([P, 256], U32, f"picked_w{i}") for i in range(2)]
+        warm_up(7, 7)
+        first_w = [sb([P, P], U32, f"first_w{jt}") for jt in range(2)]
         pick_scales(0, sb([P, 2, 256], U8, "picked_s0"))
-        pick_words(0, picked_w[0])
-        pick_words(1, picked_w[1])
-        part_words(0, picked_w[0])
-        part_words(1, picked_w[1])
-        pick_scales(1, sb([P, 2, 256], U8, "picked_s1", "picked_w0"))
-        for jt in range(4):
-            early_gate(jt, jt)
+        for jt in range(2):
+            pick_tile_words(jt, first_w[jt])
+        for jt in range(2):
+            part_tile_words(jt, first_w[jt])
+        second_w = sb([P, 256], U32, "second_w", "first_w0")
+        pick_words(1, second_w)
+        pick_scales(1, sb([P, 2, 256], U8, "picked_s1", "first_w1"))
+        part_words(1, second_w)
+        dealt_s.extend([sb([P, 2, 4, P // 4], I32, "dealt_s0", "tab_w"), sb([P, 2, 4, P // 4], I32, "dealt_s1")])
+        early_gate(0, 0)
+        early_gate(1, 1)
+        early_up(0, 2)
         pick_gate(0, 0, 512)
-        early_up(0, 4)
-        early_up(1, 5)
-        early_up(2, 6)
-        early_up(3, 7)
-        for m in range(2):
-            deal_scales(m)
-            deal_words(m)
+        deal_scales(0)
+        deal_words(0)
+        deal_scales(1)
+        shared_banks(1, 2, (3, 4))
+        early_up(2, 5)
+        early_gate(3, 2)
+        early_up(3, 6)
+        deal_words(1)
         wd_codes = [sb([P, N], U32, f"wd_codes{b}") for b in range(2)]
         wd_scales = [sb([P, N], U8, f"wd_scales{b}") for b in range(2)]
+        round_wd(0, 0, nc.scalar.copy)
         late_gate(0, (0, 1))
-        late_up(0, 2)
-        late_up(1, 3)
-        for c in range(2):
-            round_wd(0, c, nc.scalar.copy)
-        quantise_wd(0)
         pick_gate(1, 0, 512)
+        late_up(0, 7)
+        round_wd(0, 1, nc.scalar.copy)
+        turn(0, 4)
+        turn(2, 5)
+        late_up(1, 3)
+        round_wd(1, 1, nc.scalar.copy)
         round_wd_aside(1, 0)
-        round_wd(1, 1, nc.vector.tensor_copy)
-        turn(0, 0)
-        turn(2, 1)
         late_mult(0)
         late_mult(1)
-        quantise_wd(1)
+        quantise_wd(0)
         quantise_h(1, 0, 256)
+        quantise_wd(1)
         quantise_h(0, 0, 256)
-        late_gate(1, (4, 5), last_by_tile=True)
-        late_up(2, 6)
-        late_up(3, 7)
+        late_gate(1, (2, 6), last_by_tile=True)
+        late_up(2, 0)
+        late_up(3, 1)
         quantise_h(0, 256, 512)
         late_mult(2)
-        late_mult(3)
         quantise_h(1, 256, 384)
+        late_mult(3)
         quantise_h(1, 384, 512)
-        y = down(0, 256, 2)
+        y = down(0, 256, 7)
         finish(y[:, 0:1, :], 0, 1, 0, 256)
         finish(y[:, 1:2, :], 1, 2, 0, 256)
-        last_y = [bank(c, [P, 1, P]) for c in range(2)]
+        last_y = [bank(4 + c, [P, 1, P]) for c in range(2)]
         for c in range(2):
             down_pass(last_y[c][:, 0, :], c, 0, 384, 512)
         finish(down(256, 384, 3)[:], 0, 2, 256, 384)

@@ -345,7 +345,7 @@ def tile_list_gmlpt_tanh_gate_kernel(
         turn(2, 5)
         late_up(1, 3)
         round_wd(1, 1, nc.scalar.copy)
-        round_wd_aside(1, 0)
+        round_wd(1, 0, nc.vector.tensor_copy)
         late_mult(0)
         late_mult(1)
         quantise_wd(0)

@@ -306,8 +306,8 @@ def tile_list_gmlpt_tanh_gate_kernel(
         load_gate(0)
         load_words(w_late[0], 0, 1)
         load_words(w_late[1], 1, 1)
-        load_wd(0)
         load_gate(1)
+        load_wd(0)
         load_wd(1)
 
         warm_up(7, 7)
@@ -340,7 +340,7 @@ def tile_list_gmlpt_tanh_gate_kernel(
         late_gate(0, (0, 1))
         pick_gate(1, 0, 512)
         late_up(0, 7)
-        round_wd(0, 1, nc.scalar.copy)
+        round_wd(0, 1, nc.vector.tensor_copy)
         turn(0, 4)
         turn(2, 5)
         late_up(1, 3)

@@ -287,7 +287,7 @@ def tile_list_gmlpt_tanh_gate_kernel(
                     stop=(i == passes - 1),
                 )
 
-        nc.gpsimd.memset(tab_s[:], 0)
+        nc.vector.memset(tab_s[:], 0)
         nc.vector.memset(zero_in[:], 0.0)
         nc.scalar.activation(out=zero[:], in_=zero_in[:], func=TANH)
         nc.vector.memset(w_s[0][:], 0)

@@ -19,6 +19,7 @@ TANH = mybir.ActivationFunctionType.Tanh
 
 P = 128
 HALF = 512
+SCALE_LEAD = 64
 
 
 def tile_list_gmlpt_tanh_gate_kernel(
@@ -31,7 +32,11 @@ def tile_list_gmlpt_tanh_gate_kernel(
         psum = ctx.enter_context(tc.psum_pool(name="psum", bufs=1))
 
         def sb(shape, dtype, name, tag=None):
-            return keep.tile(shape, dtype, name=name, tag=tag or name, align_bytes=64)
+            return keep.tile(shape, dtype, name=name, tag=tag or name, align_bytes=256)
+
+        def plane(width, dtype, name, tag=None):
+            lead = SCALE_LEAD // (4 if dtype == I32 else 1)
+            return sb([P, lead + width], dtype, name, tag)[:, lead:]
 
         def at(offset, shape, dtype, name):
             return placed.tile(shape, dtype, name=name, offset=offset, align_bytes=64)
@@ -42,7 +47,7 @@ def tile_list_gmlpt_tanh_gate_kernel(
         offsets = keep.tile([P, J // 16], U16, name="offsets")
         tab_s = sb([P, 2, T // 4], I32, "tab_s")
         tab_w = sb([P, T], I32, "tab_w")
-        w_s = [sb([P, 2, R // 4], I32, f"w_s{m}") for m in range(2)]
+        w_s = [plane(2 * R // 4, I32, f"w_s{m}").rearrange("p (a c) -> p a c", a=2) for m in range(2)]
         wg_early = [sb([P, 1, HALF // 2], I32, f"wg_early{a}") for a in range(2)]
         wu_early = sb([P, 2, HALF // 2], I32, "wu_early")
         w_early = [[wg_early[a][:, 0, :] for a in range(2)], [wu_early[:, a, :] for a in range(2)]]
@@ -110,7 +115,7 @@ def tile_list_gmlpt_tanh_gate_kernel(
         h_rows = [sb([P, HALF], BF16, f"h_rows{jt}") for jt in range(4)]
         h_cols = [[sb([P, 2 * P, 4], BF16, f"h_cols{b}{i}") for i in range(2)] for b in range(2)]
         h_codes = sb([P, 2, J], U32, "h_codes")
-        h_scales = sb([P, 2, J], U8, "h_scales")
+        h_scales = plane(2 * J, U8, "h_scales").rearrange("p (b j) -> p b j", b=2)
         dealt_w = [[sb([P, 2, 2, P // 2], I32, f"dealt_w{m}{u}", "gate0" if (m, u) == (1, 0) else None) for u in range(2)] for m in range(2)]
         dealt_s = []
         th = {}
@@ -312,16 +317,16 @@ def tile_list_gmlpt_tanh_gate_kernel(
 
         warm_up(7, 7)
         first_w = [sb([P, P], U32, f"first_w{jt}") for jt in range(2)]
-        pick_scales(0, sb([P, 2, 256], U8, "picked_s0"))
+        pick_scales(0, plane(512, U8, "picked_s0").rearrange("p (a j) -> p a j", a=2))
         for jt in range(2):
             pick_tile_words(jt, first_w[jt])
         for jt in range(2):
             part_tile_words(jt, first_w[jt])
         second_w = sb([P, 256], U32, "second_w", "first_w0")
         pick_words(1, second_w)
-        pick_scales(1, sb([P, 2, 256], U8, "picked_s1", "first_w1"))
+        pick_scales(1, plane(512, U8, "picked_s1", "first_w1").rearrange("p (a j) -> p a j", a=2))
         part_words(1, second_w)
-        dealt_s.extend([sb([P, 2, 4, P // 4], I32, "dealt_s0", "tab_w"), sb([P, 2, 4, P // 4], I32, "dealt_s1")])
+        dealt_s.extend([plane(256, I32, name, tag).rearrange("p (a t c) -> p a t c", a=2, t=4) for name, tag in (("dealt_s0", "tab_w"), ("dealt_s1", None))])
         early_gate(0, 0)
         early_gate(1, 1)
         early_up(0, 2)
@@ -335,7 +340,7 @@ def tile_list_gmlpt_tanh_gate_kernel(
         early_up(3, 6)
         deal_words(1)
         wd_codes = [sb([P, N], U32, f"wd_codes{b}") for b in range(2)]
-        wd_scales = [sb([P, N], U8, f"wd_scales{b}") for b in range(2)]
+        wd_scales = [plane(N, U8, f"wd_scales{b}") for b in range(2)]
         round_wd(0, 0, nc.scalar.copy)
         late_gate(0, (0, 1))
         pick_gate(1, 0, 512)

@@ -121,16 +121,16 @@ def tile_list_gmlpt_tanh_gate_kernel(
         th = {}
 
         def deal_scales(m):
-            nc.vector.tensor_copy(
-                out=dealt_s[m][:].rearrange("p a t (q e) -> p a t q e", e=2),
-                in_=w_s[m][:, :, HALF // 4 :].rearrange("p a (q t e) -> p a t q e", t=4, e=2),
+            nc.scalar.copy(
+                out=dealt_s[m][:].bitcast(U32).rearrange("p a t (q e) -> p a t q e", e=2),
+                in_=w_s[m][:, :, HALF // 4 :].bitcast(U32).rearrange("p a (q t e) -> p a t q e", t=4, e=2),
             )
 
         def deal_words(m):
             for u in range(2):
-                (nc.vector, nc.gpsimd)[m].tensor_copy(
-                    out=dealt_w[m][u][:].rearrange("p a t (q e) -> p a t q e", e=4),
-                    in_=w_late[m][:].rearrange("p a (q t e) -> p a t q e", t=4, e=4)[:, :, 2 * u : 2 * u + 2],
+                (nc.scalar.copy, nc.gpsimd.tensor_copy)[m](
+                    out=dealt_w[m][u][:].bitcast(U32).rearrange("p a t (q e) -> p a t q e", e=4),
+                    in_=w_late[m][:].bitcast(U32).rearrange("p a (q t e) -> p a t q e", t=4, e=4)[:, :, 2 * u : 2 * u + 2],
                 )
 
         def early_passes(acc, m, jt, r0, r1):
@@ -326,7 +326,7 @@ def tile_list_gmlpt_tanh_gate_kernel(
         pick_words(1, second_w)
         pick_scales(1, plane(512, U8, "picked_s1", "first_w1").rearrange("p (a j) -> p a j", a=2))
         part_words(1, second_w)
-        dealt_s.extend([plane(256, I32, name, tag).rearrange("p (a t c) -> p a t c", a=2, t=4) for name, tag in (("dealt_s0", "tab_w"), ("dealt_s1", None))])
+        dealt_s.extend([plane(256, I32, name, tag).rearrange("p (a t c) -> p a t c", a=2, t=4) for name, tag in (("dealt_s0", None), ("dealt_s1", None))])
         early_gate(0, 0)
         early_gate(1, 1)
         early_up(0, 2)

@@ -279,15 +279,19 @@ def tile_list_gmlpt_tanh_gate_kernel(
                 nc.vector.tensor_tensor(out=res[:], in0=y, in1=picked_g[:, c0:c1, j0:j1], op=MULT)
             queue.dma_start(out=out_view[:, c0:c1, j0:j1], in_=res[:])
 
+        warm_in = sb([P, 4 * P], I32, "warm_in")
+        warm_codes = sb([P, 2 * P], U32, "warm_codes")
+        warm_s = plane(2 * P, U8, "warm_s")
+
         def warm_up(passes, index):
             acc = bank(index, [P, 2 * P])
             for i in range(passes):
                 nc.tensor.matmul_mx(
                     out=acc[:],
                     lhsT=w_early[0][0][:, : P // 2].bitcast(U8).bitcast(FP4X4),
-                    lhsT_scale=tab_s8[:, 0, :P],
+                    lhsT_scale=warm_s[:, :P],
                     rhs=w_early[0][0][:, :P].bitcast(U8).bitcast(FP4X4),
-                    rhs_scale=tab_s8[:, 0, : 2 * P],
+                    rhs_scale=warm_s[:],
                     start=(i == 0),
                     stop=(i == passes - 1),
                 )
@@ -295,7 +299,9 @@ def tile_list_gmlpt_tanh_gate_kernel(
         nc.vector.memset(tab_s[:], 0)
         nc.vector.memset(zero_in[:], 0.0)
         nc.scalar.activation(out=zero[:], in_=zero_in[:], func=TANH)
+        nc.vector.memset(warm_in[:], 0)
         nc.vector.memset(w_s[0][:], 0)
+        nc.vector.quantize_mx(out=warm_codes[:].bitcast(FP8X4), scales=warm_s, in_=warm_in[:].bitcast(BF16))
         nc.vector.memset(w_s[1][:], 0)
         nc.gpsimd.affine_select(
             out=ident[:], in_=zero[:], pattern=[[-1, P]], compare_op=mybir.AluOpType.not_equal, fill=1.0, base=0, channel_multiplier=1

from contextlib import ExitStack

import concourse.mybir as mybir

K, R, N, T, J = 1024, 1024, 256, 1024, 512
FLOPS = 2 * 2 * K * R * J + 2 * R * N * J

F32 = mybir.dt.float32
BF16 = mybir.dt.bfloat16
I32 = mybir.dt.int32
U32 = mybir.dt.uint32
U16 = mybir.dt.uint16
U8 = mybir.dt.uint8
FP8X4 = mybir.dt.float8_e4m3fn_x4
FP4X4 = mybir.dt.float4_e2m1fn_x4
MULT = mybir.AluOpType.mult
ADD = mybir.AluOpType.add
TANH = mybir.ActivationFunctionType.Tanh

P = 128
HALF = 512
SCALE_LEAD = 64


def tile_list_gmlpt_tanh_gate_kernel(
    tc, tab_words, tab_scales, wg_words, wg_scales, wu_words, wu_scales, wd, gT, offs, out
):
    nc = tc.nc
    with ExitStack() as ctx:
        keep = ctx.enter_context(tc.tile_pool(name="keep", bufs=1))
        placed = ctx.enter_context(tc.tile_pool(name="placed", bufs=1))
        psum = ctx.enter_context(tc.psum_pool(name="psum", bufs=1))

        def sb(shape, dtype, name, tag=None):
            return keep.tile(shape, dtype, name=name, tag=tag or name, align_bytes=256)

        def plane(width, dtype, name, tag=None):
            lead = SCALE_LEAD // (4 if dtype == I32 else 1)
            return sb([P, lead + width], dtype, name, tag)[:, lead:]

        def at(offset, shape, dtype, name):
            return placed.tile(shape, dtype, name=name, offset=offset, align_bytes=64)

        def bank(index, shape):
            return psum.tile(shape, F32, name=f"bank{index}", tag=f"bank{index}", bufs=1)

        offsets = keep.tile([P, J // 16], U16, name="offsets")
        tab_s = sb([P, 2, T // 4], I32, "tab_s")
        tab_w = sb([P, T], I32, "tab_w")
        w_s = [plane(2 * R // 4, I32, f"w_s{m}").rearrange("p (a c) -> p a c", a=2) for m in range(2)]
        wg_early = [sb([P, 1, HALF // 2], I32, f"wg_early{a}") for a in range(2)]
        wu_early = sb([P, 2, HALF // 2], I32, "wu_early")
        w_early = [[wg_early[a][:, 0, :] for a in range(2)], [wu_early[:, a, :] for a in range(2)]]
        w_late = [sb([P, 2, HALF // 2], I32, f"w_late{m}") for m in range(2)]
        gate = [sb([P, T], F32, f"gate{c}") for c in range(2)]
        wd_raw = [sb([P, 4, N], F32, f"wd_raw{b}") for b in range(2)]
        ident = sb([P, P], F32, "ident")
        zero_in = sb([P, P], F32, "zero_in")
        zero = sb([P, P], F32, "zero")

        def load_scales(dst, src):
            rows = src.bitcast(I32).rearrange("a (q r) c -> r q a c", r=4)
            for r in range(4):
                nc.sync.dma_start(out=dst[r:P:32], in_=rows[r])

        def load_words(dst, m, b, passes=slice(0, 2)):
            src = (wg_words, wu_words)[m].bitcast(I32).rearrange("a p c -> p a c")
            nc.sync.dma_start(out=dst[:], in_=src[:, passes, b * (HALF // 2) : (b + 1) * (HALF // 2)])

        def load_table():
            nc.sync.dma_start(out=tab_w[:], in_=tab_words[0].rearrange("p t d -> p (t d)").bitcast(I32))

        def load_gate(c):
            nc.sync.dma_start(out=gate[c][:], in_=gT[P * c : P * (c + 1), :])

        def load_wd(b):
            if b == 0:
                nc.sync.dma_start(out=wd_raw[0][:], in_=wd[:HALF].rearrange("(p t) n -> p t n", t=4))
            else:
                late_rows = wd[HALF:].rearrange("(q t i) n -> t q i n", t=4, i=8)
                for t in range(4):
                    nc.sync.dma_start(out=wd_raw[1][:, t, :], in_=late_rows[t])

        tab_s8 = tab_s[:].bitcast(U8)

        def lst(j0, j1):
            return offsets[:, j0 // 16 : j1 // 16]

        stat_w, stat_s = {}, {}
        parted = [sb([P, 2, 4 * P], U8, f"parted{i}") for i in range(2)]
        pair_s = {}

        def pick_scales(i, picked):
            pair_s[i] = picked
            for a in range(2):
                nc.vector.tensor_copy(out=picked[:, a, :], in_=tab_s8[:, a, :].indirect(lst(256 * i, 256 * (i + 1))))
            for jt in (2 * i, 2 * i + 1):
                stat_s[jt] = picked[:, :, P * (jt % 2) : P * (jt % 2 + 1)]

        def pick_words(i, words):
            for jt in (2 * i, 2 * i + 1):
                stat_w[jt] = parted[i][:, :, 2 * P * (jt % 2) : 2 * P * (jt % 2 + 1)]
            nc.vector.tensor_copy(out=words[:], in_=tab_w[:].bitcast(U32).indirect(lst(256 * i, 256 * (i + 1))))

        def part_words(i, words):
            nc.vector.tensor_copy(out=parted[i][:].bitcast(U16), in_=words[:].bitcast(U16).rearrange("p (j d) -> p d j", d=2))

        def pick_tile_words(jt, words):
            stat_w[jt] = parted[jt // 2][:, :, 2 * P * (jt % 2) : 2 * P * (jt % 2 + 1)]
            nc.vector.tensor_copy(out=words[:], in_=tab_w[:].bitcast(U32).indirect(lst(P * jt, P * (jt + 1))))

        def part_tile_words(jt, words):
            nc.vector.tensor_copy(out=stat_w[jt].bitcast(U16), in_=words[:].bitcast(U16).rearrange("p (j d) -> p d j", d=2))

        h_rows = [sb([P, HALF], BF16, f"h_rows{jt}") for jt in range(4)]
        h_cols = [[sb([P, 2 * P, 4], BF16, f"h_cols{b}{i}") for i in range(2)] for b in range(2)]
        h_codes = sb([P, 2, J], U32, "h_codes")
        h_scales = plane(2 * J, U8, "h_scales").rearrange("p (b j) -> p b j", b=2)
        dealt_w = [[sb([P, 2, 2, P // 2], I32, f"dealt_w{m}{u}", "gate0" if (m, u) == (1, 0) else None) for u in range(2)] for m in range(2)]
        dealt_s = []
        th = {}

        def deal_scales(m):
            nc.scalar.copy(
                out=dealt_s[m][:].bitcast(U32).rearrange("p a t (q e) -> p a t q e", e=2),
                in_=w_s[m][:, :, HALF // 4 :].bitcast(U32).rearrange("p a (q t e) -> p a t q e", t=4, e=2),
            )

        def deal_words(m):
            for u in range(2):
                (nc.scalar.copy, nc.gpsimd.tensor_copy)[m](
                    out=dealt_w[m][u][:].bitcast(U32).rearrange("p a t (q e) -> p a t q e", e=4),
                    in_=w_late[m][:].bitcast(U32).rearrange("p a (q t e) -> p a t q e", t=4, e=4)[:, :, 2 * u : 2 * u + 2],
                )

        def early_passes(acc, m, jt, r0, r1):
            for a in range(2):
                nc.tensor.matmul_mx(
                    out=acc,
                    lhsT=stat_w[jt][:, a, :].bitcast(FP4X4),
                    lhsT_scale=stat_s[jt][:, a, :],
                    rhs=w_early[m][a][:, r0 // 2 : r1 // 2].bitcast(U8).bitcast(FP4X4),
                    rhs_scale=w_s[m][:].bitcast(U8)[:, a, r0:r1],
                    start=(a == 0),
                    stop=(a == 1),
                )
            return acc.rearrange("j (p u e) -> j u p e", u=2, e=2)

        def early_product(m, jt, index):
            return early_passes(bank(index, [P, HALF])[:], m, jt, 0, HALF)

        def shared_banks(up_jt, gate_jt, indices):
            both = [bank(index, [P, 2, HALF // 2]) for index in indices]
            ub = [early_passes(both[h][:, 0, :], 1, up_jt, 256 * h, 256 * (h + 1)) for h in range(2)]
            ga = [early_passes(both[h][:, 1, :], 0, gate_jt, 256 * h, 256 * (h + 1)) for h in range(2)]
            th[gate_jt, 0] = sb([P, 2, P, 2], F32, f"th{gate_jt}0")
            rows = h_rows[up_jt][:].rearrange("j (u p e) -> j u p e", u=2, e=2)
            for h in range(2):
                part = slice(64 * h, 64 * (h + 1))
                nc.scalar.activation(out=th[gate_jt, 0][:, :, part, :], in_=ga[h], func=TANH)
                nc.vector.tensor_tensor(out=rows[:, :, part, :], in0=ub[h], in1=th[up_jt, 0][:, :, part, :], op=MULT)

        def early_gate(jt, index):
            ga = early_product(0, jt, index)
            th[jt, 0] = sb([P, 2, P, 2], F32, f"th{jt}0")
            nc.scalar.activation(out=th[jt, 0][:], in_=ga, func=TANH)

        def early_up(jt, index, aside=False):
            ub = early_product(1, jt, index)
            rows = h_rows[jt][:].rearrange("j (u p e) -> j u p e", u=2, e=2)
            if aside:
                ub_sb = sb([P, 2, P, 2], F32, f"ub_sb{jt}")
                nc.scalar.copy(out=ub_sb[:], in_=ub)
                nc.gpsimd.tensor_tensor(out=rows, in0=ub_sb[:], in1=th[jt, 0][:], op=MULT)
            else:
                nc.vector.tensor_tensor(out=rows, in0=ub, in1=th[jt, 0][:], op=MULT)

        def late_pass(out_ap, m, t, words, scales):
            for a in range(2):
                nc.tensor.matmul_mx(
                    out=out_ap,
                    lhsT=dealt_w[m][t // 2][:, a, t % 2, :].bitcast(U8).bitcast(FP4X4),
                    lhsT_scale=dealt_s[m][:, a, t, :].bitcast(U8),
                    rhs=words[:, a, :].bitcast(FP4X4),
                    rhs_scale=scales[:, a, :],
                    start=(a == 0),
                    stop=(a == 1),
                )

        def late_gate(i, indices, last_by_tile=False):
            th[i, 1] = sb([P, 4, 2 * P], F32, f"th{i}1")
            for u in range(2):
                ga = bank(indices[u], [P, 2, 2 * P])
                for e in range(2):
                    late_pass(ga[:, e, :], 0, 2 * u + e, parted[i][:], pair_s[i][:])
                for j0, j1 in ((0, P), (P, 2 * P)) if last_by_tile and u == 1 else ((0, 2 * P),):
                    nc.scalar.activation(out=th[i, 1][:, 2 * u : 2 * u + 2, j0:j1], in_=ga[:, :, j0:j1], func=TANH)

        ub_late = {}

        def late_up(jt, index):
            ub_late[jt] = bank(index, [P, 4, P])
            for t in range(4):
                late_pass(ub_late[jt][:, t, :], 1, t, stat_w[jt], stat_s[jt])

        def late_mult(jt):
            nc.vector.tensor_tensor(
                out=h_cols[1][jt // 2][:, P * (jt % 2) : P * (jt % 2 + 1), :].rearrange("p (c i) t -> p c t i", i=2),
                in0=ub_late[jt][:].rearrange("p t (c i) -> p c t i", i=2),
                in1=th[jt // 2, 1][:, :, P * (jt % 2) : P * (jt % 2 + 1)].rearrange("p t (c i) -> p c t i", i=2),
                op=MULT,
            )

        def turn(jt0, index):
            turned = bank(index, [P, 2, 2, P])
            for jt in range(jt0, jt0 + 2):
                words = h_rows[jt][:].bitcast(F32)
                for u in range(2):
                    nc.tensor.transpose(turned[:, jt - jt0, u, :], words[:, P * u : P * (u + 1)], ident[:])
            nc.scalar.copy(
                out=h_cols[0][jt0 // 2][:].bitcast(F32).rearrange("p (i c k) u -> p i c u k", i=2, k=2),
                in_=turned[:].rearrange("p i u (c k) -> p i c u k", k=2),
            )

        def quantise_h(b, j0, j1):
            nc.vector.quantize_mx(
                out=h_codes[:, b, j0:j1].bitcast(FP8X4),
                scales=h_scales[:, b, j0:j1],
                in_=h_cols[b][j0 // 256][:, j0 % 256 : j0 % 256 + j1 - j0, :].rearrange("p j t -> p (j t)"),
            )

        wd_bf = [sb([P, N, 4], BF16, f"wd_bf{b}") for b in range(2)]

        def round_wd(b, c, copy):
            cols = slice(P * c, P * (c + 1))
            copy(out=wd_bf[b][:, cols, :].rearrange("p (c i) t -> p c t i", i=2), in_=wd_raw[b][:, :, cols].rearrange("p t (c i) -> p c t i", i=2))

        def round_wd_aside(b, c):
            cols = slice(P * c, P * (c + 1))
            nc.gpsimd.tensor_scalar(
                out=wd_bf[b][:, cols, :], in0=wd_raw[b][:, :, cols].rearrange("p t n -> p n t"), scalar1=1.0, scalar2=0.0, op0=MULT, op1=ADD
            )

        def quantise_wd(b):
            nc.vector.quantize_mx(out=wd_codes[b][:].bitcast(FP8X4), scales=wd_scales[b][:], in_=wd_bf[b][:].rearrange("p n t -> p (n t)"))

        picked_g = sb([P, 2, J], F32, "picked_g")

        def pick_gate(c, j0, j1):
            nc.vector.tensor_copy(out=picked_g[:, c, j0:j1], in_=gate[c][:].indirect(lst(j0, j1)))

        out_view = out.rearrange("(c p) j -> p c j", c=2)

        def down_pass(y, c, b, j0, j1):
            nc.tensor.matmul_mx(
                out=y,
                lhsT=wd_codes[b][:, P * c : P * (c + 1)].bitcast(FP8X4),
                lhsT_scale=wd_scales[b][:, P * c : P * (c + 1)],
                rhs=h_codes[:, b, j0:j1].bitcast(FP8X4),
                rhs_scale=h_scales[:, b, j0:j1],
                start=(b == 0),
                stop=(b == 1),
            )

        def down(j0, j1, index):
            y = bank(index, [P, 2, j1 - j0])
            for c in range(2):
                for b in range(2):
                    down_pass(y[:, c, :], c, b, j0, j1)
            return y

        def finish(y, c0, c1, j0, j1, aside=False, queue=nc.sync, tag=None):
            res = sb([P, c1 - c0, j1 - j0], F32, f"res{c0}_{j0}", tag)
            if aside:
                y_sb = sb([P, c1 - c0, j1 - j0], F32, f"y_sb{c0}_{j0}")
                nc.scalar.copy(out=y_sb[:], in_=y)
                nc.gpsimd.tensor_tensor(out=res[:], in0=y_sb[:], in1=picked_g[:, c0:c1, j0:j1], op=MULT)
            else:
                nc.vector.tensor_tensor(out=res[:], in0=y, in1=picked_g[:, c0:c1, j0:j1], op=MULT)
            queue.dma_start(out=out_view[:, c0:c1, j0:j1], in_=res[:])

        warm_in = sb([P, 4 * P], I32, "warm_in")
        warm_codes = sb([P, 2 * P], U32, "warm_codes")
        warm_s = plane(2 * P, U8, "warm_s")

        def warm_up(passes, index):
            acc = bank(index, [P, 2 * P])
            for i in range(passes):
                nc.tensor.matmul_mx(
                    out=acc[:],
                    lhsT=w_early[0][0][:, : P // 2].bitcast(U8).bitcast(FP4X4),
                    lhsT_scale=warm_s[:, :P],
                    rhs=w_early[0][0][:, :P].bitcast(U8).bitcast(FP4X4),
                    rhs_scale=warm_s[:],
                    start=(i == 0),
                    stop=(i == passes - 1),
                )

        nc.vector.memset(tab_s[:], 0)
        nc.vector.memset(zero_in[:], 0.0)
        nc.scalar.activation(out=zero[:], in_=zero_in[:], func=TANH)
        nc.vector.memset(warm_in[:], 0)
        nc.vector.memset(w_s[0][:], 0)
        nc.vector.quantize_mx(out=warm_codes[:].bitcast(FP8X4), scales=warm_s, in_=warm_in[:].bitcast(BF16))
        nc.vector.memset(w_s[1][:], 0)
        nc.gpsimd.affine_select(
            out=ident[:], in_=zero[:], pattern=[[-1, P]], compare_op=mybir.AluOpType.not_equal, fill=1.0, base=0, channel_multiplier=1
        )
        nc.sync.dma_start(offsets[:], offs)
        load_words(wg_early[0], 0, 0, slice(0, 1))
        load_scales(tab_s, tab_scales)
        load_table()
        load_words(wg_early[1], 0, 0, slice(1, 2))
        load_scales(w_s[0], wg_scales)
        load_words(wu_early, 1, 0)
        load_scales(w_s[1], wu_scales)
        load_gate(0)
        load_words(w_late[0], 0, 1)
        load_words(w_late[1], 1, 1)
        load_gate(1)
        load_wd(0)
        load_wd(1)

        warm_up(7, 7)
        first_w = [sb([P, P], U32, f"first_w{jt}") for jt in range(2)]
        pick_scales(0, plane(512, U8, "picked_s0").rearrange("p (a j) -> p a j", a=2))
        for jt in range(2):
            pick_tile_words(jt, first_w[jt])
        for jt in range(2):
            part_tile_words(jt, first_w[jt])
        second_w = sb([P, 256], U32, "second_w", "first_w0")
        pick_words(1, second_w)
        pick_scales(1, plane(512, U8, "picked_s1", "first_w1").rearrange("p (a j) -> p a j", a=2))
        part_words(1, second_w)
        dealt_s.extend([plane(256, I32, name, tag).rearrange("p (a t c) -> p a t c", a=2, t=4) for name, tag in (("dealt_s0", None), ("dealt_s1", None))])
        early_gate(0, 0)
        early_gate(1, 1)
        early_up(0, 2)
        pick_gate(0, 0, 512)
        deal_scales(0)
        deal_words(0)
        deal_scales(1)
        shared_banks(1, 2, (3, 4))
        early_up(2, 5)
        early_gate(3, 2)
        early_up(3, 6)
        deal_words(1)
        wd_codes = [sb([P, N], U32, f"wd_codes{b}") for b in range(2)]
        wd_scales = [plane(N, U8, f"wd_scales{b}") for b in range(2)]
        round_wd(0, 0, nc.scalar.copy)
        late_gate(0, (0, 1))
        pick_gate(1, 0, 512)
        late_up(0, 7)
        round_wd(0, 1, nc.vector.tensor_copy)
        turn(0, 4)
        turn(2, 5)
        late_up(1, 3)
        round_wd(1, 1, nc.scalar.copy)
        round_wd(1, 0, nc.vector.tensor_copy)
        late_mult(0)
        late_mult(1)
        quantise_wd(0)
        quantise_h(1, 0, 256)
        quantise_wd(1)
        quantise_h(0, 0, 256)
        late_gate(1, (2, 6), last_by_tile=True)
        late_up(2, 0)
        late_up(3, 1)
        quantise_h(0, 256, 512)
        late_mult(2)
        quantise_h(1, 256, 384)
        late_mult(3)
        quantise_h(1, 384, 512)
        y = down(0, 256, 7)
        finish(y[:, 0:1, :], 0, 1, 0, 256)
        finish(y[:, 1:2, :], 1, 2, 0, 256)
        last_y = [bank(4 + c, [P, 1, P]) for c in range(2)]
        for c in range(2):
            down_pass(last_y[c][:, 0, :], c, 0, 384, 512)
        finish(down(256, 384, 3)[:], 0, 2, 256, 384)
        for c in range(2):
            down_pass(last_y[c][:, 0, :], c, 1, 384, 512)
            finish(last_y[c][:], c, c + 1, 384, 512)
